import numpy as np
import ml_dtypes


def mxq(x, axis, fmt="e4m3"):
    dtype, down = {"e4m3": (ml_dtypes.float8_e4m3fn, 7), "e5m2": (ml_dtypes.float8_e5m2, 14)}[fmt]
    v = np.moveaxis(np.asarray(x, np.float32).astype(ml_dtypes.bfloat16).astype(np.float64), axis, -1)
    blocks = v.reshape(v.shape[:-1] + (-1, 32))
    amax = np.abs(blocks).max(-1, keepdims=True)
    byte = np.maximum(np.where(amax > 0, np.frexp(amax)[1] - 1 + 127, 0) - down, 1)
    scale = np.exp2(byte - 127.0)
    codes = (blocks / scale).astype(np.float32).astype(dtype).astype(np.float64)
    return np.moveaxis((codes * scale).reshape(v.shape), -1, axis)


WIDE = False


def mx_kscale(k):
    if not WIDE:
        return np.ones(k)
    levels = np.array([10, -10, 5, -5, 0])
    if k % 512:
        return np.exp2(np.random.permutation(np.resize(levels, k // 32))).repeat(32)
    a = np.empty((k // 512, 16))
    for p in range(k // 512):
        a[p, :8] = np.random.permutation(np.resize(levels, 8))
        for g in range(8):
            far = levels[np.abs(levels - a[p, g]) >= 10]
            a[p, g + 8] = far[np.random.randint(len(far))]
    return np.exp2(a.ravel()).repeat(32)


def f64(x):
    return np.asarray(x).astype(np.float64)


def striped8(idx):
    return np.concatenate([x.reshape(-1, 16).T for x in idx]).astype(np.uint16)


def runs(offs, k):
    lists = np.stack([offs[16 * r : 16 * r + 16].T.reshape(-1) for r in range(8)]).astype(np.int64)
    return lists[np.arange(k) % 512 // 64]


def pack_weight(w):
    k, n = w.shape
    w = f64(np.asarray(w, np.float32).astype(ml_dtypes.bfloat16)).reshape(k // 32, 32, n)
    amax = np.abs(w).max(1)
    byte = np.clip(np.where(amax > 0, np.frexp(amax)[1] - 1 + 127 - 7, 1), 1, 254)
    scaled = (w * np.exp2(127.0 - byte)[:, None, :]).reshape(k, n).astype(np.float32)
    words = np.ascontiguousarray(scaled.reshape(k // 512, 128, 4, n).transpose(0, 1, 3, 2)).astype(ml_dtypes.float8_e4m3fn).view(np.uint8)
    return words, np.ascontiguousarray(byte.astype(np.uint8).reshape(k // 512, 16, n))


def unpack_weight(words, scales):
    g, p, n, _ = words.shape
    vals = np.ascontiguousarray(words).view(ml_dtypes.float8_e4m3fn).astype(np.float64) * np.repeat(np.exp2(scales.astype(np.float64) - 127.0), 8, axis=1)[..., None]
    return vals.transpose(0, 1, 3, 2).reshape(g * 512, n)

def planes(y):
    n, m = y.shape
    v = y.astype(np.float32).astype(ml_dtypes.bfloat16).astype(np.float64).reshape(n // 32, 32, m)
    top = np.abs(v).max(1)
    byte = np.clip(np.where(top > 0, np.frexp(top)[1] - 1 + 127 - 7, 1), 1, 254)
    codes = (v * np.exp2(127.0 - byte)[:, None, :]).reshape(n, m).astype(np.float32).astype(ml_dtypes.float8_e4m3fn).view(np.uint8)
    words = codes.reshape(n // 512, 128, 4, m).transpose(0, 1, 3, 2)
    return np.ascontiguousarray(words), np.ascontiguousarray(byte.astype(np.uint8).reshape(n // 512, 16, m))


K, T, S, V, N, H = 512, 2048, 512, 256, 512, 512


def setup_inputs():
    n = np.random.standard_normal
    s = mx_kscale(K)[:, None]
    u = mx_kscale(S)
    packed_xT = pack_weight(n((K, T)) * s)
    return {
        "x_words": packed_xT[0],
        "x_scales": packed_xT[1],
        "wa": (n((K, H)) / np.sqrt(K) / s).astype(np.float32),
        "wb": (n((K, N)) / np.sqrt(K) / s).astype(np.float32),
        "gt": (np.random.uniform(0.5, 1.5, (S, 1)) * u[:, None]).astype(np.float32),
        "gi": (np.random.uniform(0.5, 1.5, (S, 1)) / u[:, None]).astype(np.float32),
        "offs": striped8(np.stack([np.random.permutation(T)[:S] for _ in range(8)])),
        "cols": striped8(np.stack([np.random.permutation(N)[:V] for _ in range(8)])),
    }


def reference(x_words, x_scales, wa, wb, gt, gi, offs, cols):
    xq = unpack_weight(x_words, x_scales)[np.arange(K)[:, None], runs(offs, K)]
    a = xq.T @ mxq(f64(wa), 0, "e4m3")
    z = f64(gt) * a
    b = xq.T @ mxq(f64(wb), 0, "e4m3")
    z2 = f64(gi) * b
    cv = 0.0625 * ((mxq(z, 0, "e4m3").T @ mxq(z2, 0, "e4m3")))
    out_0 = np.tanh(cv[np.arange(H)[:, None], runs(cols, H)])
    return (out_0,) + planes(out_0)

@@ -1,0 +1,213 @@
+from contextlib import ExitStack
+
+import concourse.mybir as mybir
+
+K, T, S, V, N, H = 512, 2048, 512, 256, 512, 512
+FLOPS = 2 * K * S * H + 2 * K * S * N + 2 * S * H * N
+
+F32 = mybir.dt.float32
+BF16 = mybir.dt.bfloat16
+I32 = mybir.dt.int32
+U32 = mybir.dt.uint32
+U16 = mybir.dt.uint16
+U8 = mybir.dt.uint8
+FP8X4 = mybir.dt.float8_e4m3fn_x4
+TANH = mybir.ActivationFunctionType.Tanh
+MULT = mybir.AluOpType.mult
+
+P = 128
+PACK = 4
+HALF = 256
+
+
+def tile_picked_selmom_none_po_kernel(
+    tc, x_words, x_scales, wa, wb, gt, gi, offs, cols, out_0, out_1, out_2
+):
+    nc = tc.nc
+    with ExitStack() as ctx:
+        keep = ctx.enter_context(tc.tile_pool(name="keep", bufs=1))
+        psum = ctx.enter_context(tc.psum_pool(name="psum", bufs=4))
+
+        def sb(name, shape, dtype, tag=None):
+            return keep.tile(shape, dtype, name=name, tag=tag or name, align_bytes=64)
+
+        offs_t = sb("offs_t", [P, S // 16], U16)
+        cols_t = sb("cols_t", [P, V // 16], U16)
+        nc.sync.dma_start(offs_t[:], offs)
+        nc.sync.dma_start(cols_t[:], cols)
+
+        gt_t = sb("gt_t", [P, PACK], F32)
+        gi_t = sb("gi_t", [P, PACK], F32)
+        nc.scalar.dma_start(gi_t[:], gi.rearrange("(p s) o -> p (s o)", s=PACK))
+        nc.scalar.dma_start(gt_t[:], gt.rearrange("(p s) o -> p (s o)", s=PACK))
+
+        xs = sb("xs", [P, T], U8, tag="bytes_then_words")
+        nc.vector.memset(xs[:].bitcast(I32), 0)
+        nc.scalar.dma_start(xs[0:P:8, :].bitcast(I32), x_scales[0].bitcast(I32))
+
+        zero = sb("zero", [P, 1], F32)
+        bias = sb("bias", [P, 1], F32)
+        nc.vector.memset(zero[:], 0.0)
+        nc.scalar.activation(bias[:], zero[:], TANH)
+
+        xw = sb("xw", [P, T], U32, tag="words_then_codes")
+        nc.sync.dma_start(xw[:].bitcast(I32), x_words[0].rearrange("p c r -> p (c r)").bitcast(I32))
+
+        wb_rows = wb.rearrange("(p j) c -> p j c", j=PACK)
+        wa_rows = wa.rearrange("(p j) c -> p j c", j=PACK)
+        wb_first = sb("wb_first", [P, PACK * HALF], F32)
+        nc.sync.dma_start(wb_first[:].rearrange("p (j c) -> p j c", j=PACK), wb_rows[:, :, 0:HALF])
+
+        gs = sb("gs", [P, S], U8, tag="bytes_then_weights")
+        ds = sb("ds", [P, S], U8)
+        nc.vector.tensor_copy(gs[:], xs[:].indirect(offs_t[:]))
+        nc.vector.tensor_copy(
+            ds[:].rearrange("p (s m) -> p m s", s=PACK), gs[:].rearrange("p (m s) -> p m s", s=PACK)
+        )
+        for a in range(1, 4):
+            nc.sync.dma_start(ds[a:P:32, :].bitcast(I32), ds[8 * a : P : 32, :].bitcast(I32))
+
+        late = sb("late", [P, 3 * PACK * HALF], F32, tag="bytes_then_weights")
+        pieces = [late[:, i * PACK * HALF : (i + 1) * PACK * HALF].rearrange("p (j c) -> p j c", j=PACK) for i in range(3)]
+        nc.sync.dma_start(pieces[0], wb_rows[:, :, HALF:N])
+        nc.sync.dma_start(pieces[1], wa_rows[:, :, 0:HALF])
+        nc.sync.dma_start(pieces[2], wa_rows[:, :, HALF:H])
+        wb_raw = [wb_first[:].rearrange("p (j c) -> p j c", j=PACK), pieces[0]]
+        wa_raw = pieces[1:]
+
+        gw = sb("gw", [P, S], U32, tag="bytes_then_words")
+        dw = sb("dw", [P, S], U32)
+        nc.vector.tensor_copy(gw[:], xw[:].indirect(offs_t[:]))
+        nc.vector.tensor_copy(
+            dw[:].bitcast(I32).rearrange("p (s m) -> p m s", s=PACK),
+            gw[:].bitcast(I32).rearrange("p (m s) -> p m s", s=PACK),
+        )
+
+        def project(codes, scales, c):
+            acc = psum.tile([P, PACK, P], F32, name=c[0])
+            for s in range(PACK):
+                nc.tensor.matmul_mx(
+                    out=acc[:, s, :],
+                    lhsT=dw[:, s * P : (s + 1) * P].bitcast(FP8X4),
+                    lhsT_scale=ds[:, s * P : (s + 1) * P],
+                    rhs=codes[:, c[1] * P : (c[1] + 1) * P].bitcast(FP8X4),
+                    rhs_scale=scales[:, c[1] * P : (c[1] + 1) * P],
+                    start=True,
+                    stop=True,
+                )
+            return acc
+
+        def weigh(dst, acc, gate):
+            nc.vector.tensor_tensor(
+                dst,
+                acc[:].rearrange("p s m -> p m s"),
+                gate[:].rearrange("p (o s) -> p o s", o=1).broadcast_to([P, P, PACK]),
+                MULT,
+            )
+
+        wb_bf = [
+            sb("wb_bf0", [P, P * PACK], BF16),
+            sb("wb_bf1", [P, P * PACK], BF16, tag="bytes_then_words"),
+            sb("wb_bf2", [P, HALF * PACK], BF16),
+        ]
+        wb_c = sb("wb_c", [P, N], U32, tag="words_then_codes")
+        wb_s = sb("wb_s", [P, N], U8)
+        z2_bf = sb("z2_bf", [P, N * PACK], BF16)
+        z2_c = sb("z2_c", [P, N], U32)
+        z2_s = sb("z2_s", [P, N], U8)
+
+        def weave(eng, dst, lo, hi):
+            h = lo // HALF
+            eng(
+                dst[:].rearrange("p (c i j) -> p c j i", i=4, j=PACK),
+                wb_raw[h][:, :, lo - h * HALF : hi - h * HALF].rearrange("p j (c i) -> p c j i", i=4),
+            )
+
+        def quant(codes, scales, src, lo, hi):
+            nc.vector.quantize_mx(
+                out=codes[:, lo:hi].bitcast(FP8X4), scales=scales[:, lo:hi], in_=src
+            )
+
+        def second(c):
+            acc = project(wb_c, wb_s, ("early", c))
+            weigh(z2_bf[:, c * P * PACK : (c + 1) * P * PACK].rearrange("p (m s) -> p m s", s=PACK), acc, gi_t)
+
+        weave(nc.scalar.copy, wb_bf[0], 0, P)
+        weave(nc.vector.tensor_copy, wb_bf[1], P, HALF)
+        quant(wb_c, wb_s, wb_bf[0][:], 0, P)
+        quant(wb_c, wb_s, wb_bf[1][:], P, HALF)
+        weave(nc.scalar.copy, wb_bf[2], HALF, N)
+        second(0)
+        second(1)
+        quant(wb_c, wb_s, wb_bf[2][:], HALF, N)
+        quant(z2_c, z2_s, z2_bf[:, 0 : HALF * PACK], 0, HALF)
+        second(2)
+        second(3)
+        quant(z2_c, z2_s, z2_bf[:, HALF * PACK : N * PACK], HALF, N)
+
+        wa_bf = sb("wa_bf", [P, H * PACK], BF16)
+        wa_c = sb("wa_c", [P, H], U32)
+        wa_s = sb("wa_s", [P, H], U8)
+        wa_view = wa_bf[:].rearrange("p (t m j) -> p m j t", t=PACK, j=PACK)
+        for h in range(2):
+            nc.scalar.copy(
+                wa_view[:, h * 64 : (h + 1) * 64, :, :], wa_raw[h].rearrange("p j (m t) -> p m j t", t=PACK)
+            )
+        z_bf = sb("z_bf", [P, H * PACK], BF16)
+        z_c = sb("z_c", [P, H], U32)
+        z_s = sb("z_s", [P, H], U8)
+        y = sb("y", [P, PACK, V], F32)
+        out_rows = out_0.rearrange("(p t) v -> p t v", t=PACK)
+        accs = []
+        for t in range(PACK):
+            part = slice(t * P * PACK, (t + 1) * P * PACK)
+            colr = slice(t * P, (t + 1) * P)
+            nc.vector.quantize_mx(out=wa_c[:, colr].bitcast(FP8X4), scales=wa_s[:, colr], in_=wa_bf[:, part])
+            accs.append(project(wa_c, wa_s, ("late", t)))
+        wins = []
+
+        def first(t):
+            weigh(z_bf[:, t * P * PACK : (t + 1) * P * PACK].rearrange("p (m s) -> p m s", s=PACK), accs[t], gt_t)
+
+        def moments(t):
+            colr = slice(t * P, (t + 1) * P)
+            quant(z_c, z_s, z_bf[:, t * P * PACK : (t + 1) * P * PACK], t * P, (t + 1) * P)
+            cv = psum.tile([P, N], F32, name="early")
+            nc.tensor.matmul_mx(
+                out=cv[:],
+                lhsT=z_c[:, colr].bitcast(FP8X4),
+                lhsT_scale=z_s[:, colr],
+                rhs=z2_c[:].bitcast(FP8X4),
+                rhs_scale=z2_s[:],
+                start=True,
+                stop=True,
+            )
+            win = sb("win%d" % t, [P, N], F32)
+            nc.scalar.activation(win[:], cv[:], TANH, bias=bias[:], scale=0.0625)
+            wins.append(win)
+
+        def fetch(t):
+            nc.vector.tensor_copy(y[:, t, :], wins[t][:].indirect(cols_t[:]))
+            nc.sync.dma_start(out_rows[:, t, :], y[:, t, :])
+
+        first(0)
+        for t in range(1, PACK):
+            first(t)
+            moments(t - 1)
+        fetch(0)
+        moments(PACK - 1)
+        for t in range(1, PACK):
+            fetch(t)
+
+        y_bf = sb("y_bf", [P, V * PACK], BF16)
+        y_c = sb("y_c", [P, V], U32)
+        y_s = sb("y_s", [P, V], U8)
+        y_dst = y_bf[:].rearrange("p (c i t) -> p c t i", i=4, t=PACK)
+        y_src = y[:].rearrange("p t (c i) -> p c t i", i=4)
+        nc.vector.tensor_copy(y_dst[:, 0:44], y_src[:, 0:44])
+        nc.scalar.copy(y_dst[:, 44:64], y_src[:, 44:64])
+        nc.vector.quantize_mx(out=y_c[:].bitcast(FP8X4), scales=y_s[:], in_=y_bf[:])
+        nc.sync.dma_start(out_1[0].rearrange("p c r -> p (c r)").bitcast(I32), y_c[:].bitcast(I32))
+        for q in range(4):
+            eng = nc.scalar if q % 2 == 0 else nc.sync
+            eng.dma_start(out_2[0][4 * q : 4 * q + 4, :].bitcast(I32), y_s[32 * q : 32 * q + 4, :].bitcast(I32))

@@ -13,6 +13,7 @@ U16 = mybir.dt.uint16
 U8 = mybir.dt.uint8
 FP8X4 = mybir.dt.float8_e4m3fn_x4
 TANH = mybir.ActivationFunctionType.Tanh
+COPY = mybir.ActivationFunctionType.Copy
 MULT = mybir.AluOpType.mult
 
 P = 128
@@ -26,6 +27,7 @@ def tile_picked_selmom_none_po_kernel(
     nc = tc.nc
     with ExitStack() as ctx:
         keep = ctx.enter_context(tc.tile_pool(name="keep", bufs=1))
+        shared = ctx.enter_context(tc.tile_pool(name="shared", bufs=1))
         psum = ctx.enter_context(tc.psum_pool(name="psum", bufs=4))
 
         def sb(name, shape, dtype, tag=None):
@@ -34,16 +36,17 @@ def tile_picked_selmom_none_po_kernel(
         offs_t = sb("offs_t", [P, S // 16], U16)
         cols_t = sb("cols_t", [P, V // 16], U16)
         nc.sync.dma_start(offs_t[:], offs)
+        xs = sb("xs", [P, T], U8, tag="bytes_then_words")
+        nc.sync.dma_start(
+            xs[:].bitcast(I32),
+            x_scales[0].bitcast(I32).rearrange("q (o c) -> q o c", o=1).broadcast_to([16, 8, T // 4]),
+        )
         nc.sync.dma_start(cols_t[:], cols)
 
         gt_t = sb("gt_t", [P, PACK], F32)
         gi_t = sb("gi_t", [P, PACK], F32)
         nc.scalar.dma_start(gi_t[:], gi.rearrange("(p s) o -> p (s o)", s=PACK))
         nc.scalar.dma_start(gt_t[:], gt.rearrange("(p s) o -> p (s o)", s=PACK))
-
-        xs = sb("xs", [P, T], U8, tag="bytes_then_words")
-        nc.vector.memset(xs[:].bitcast(I32), 0)
-        nc.scalar.dma_start(xs[0:P:8, :].bitcast(I32), x_scales[0].bitcast(I32))
 
         zero = sb("zero", [P, 1], F32)
         bias = sb("bias", [P, 1], F32)
@@ -55,32 +58,33 @@ def tile_picked_selmom_none_po_kernel(
 
         wb_rows = wb.rearrange("(p j) c -> p j c", j=PACK)
         wa_rows = wa.rearrange("(p j) c -> p j c", j=PACK)
-        wb_first = sb("wb_first", [P, PACK * HALF], F32)
-        nc.sync.dma_start(wb_first[:].rearrange("p (j c) -> p j c", j=PACK), wb_rows[:, :, 0:HALF])
+        wb_raw = []
+        for h in range(2):
+            raw = sb("wb_raw%d" % h, [P, PACK * HALF], F32)
+            wb_raw.append(raw[:].rearrange("p (j c) -> p j c", j=PACK))
+            nc.sync.dma_start(wb_raw[h], wb_rows[:, :, h * HALF : (h + 1) * HALF])
 
-        gs = sb("gs", [P, S], U8, tag="bytes_then_weights")
+        gs = shared.tile([P, S], U8, name="gs", offset=4096 - S // 2)
         ds = sb("ds", [P, S], U8)
         nc.vector.tensor_copy(gs[:], xs[:].indirect(offs_t[:]))
         nc.vector.tensor_copy(
-            ds[:].rearrange("p (s m) -> p m s", s=PACK), gs[:].rearrange("p (m s) -> p m s", s=PACK)
+            ds[:].rearrange("p (s c i) -> p c s i", s=PACK, i=16), gs[:].rearrange("p (c i s) -> p c s i", s=PACK, i=16)
         )
         for a in range(1, 4):
             nc.sync.dma_start(ds[a:P:32, :].bitcast(I32), ds[8 * a : P : 32, :].bitcast(I32))
 
-        late = sb("late", [P, 3 * PACK * HALF], F32, tag="bytes_then_weights")
-        pieces = [late[:, i * PACK * HALF : (i + 1) * PACK * HALF].rearrange("p (j c) -> p j c", j=PACK) for i in range(3)]
-        nc.sync.dma_start(pieces[0], wb_rows[:, :, HALF:N])
-        nc.sync.dma_start(pieces[1], wa_rows[:, :, 0:HALF])
-        nc.sync.dma_start(pieces[2], wa_rows[:, :, HALF:H])
-        wb_raw = [wb_first[:].rearrange("p (j c) -> p j c", j=PACK), pieces[0]]
-        wa_raw = pieces[1:]
+        wa_raw = []
+        for h in range(2):
+            raw = shared.tile([P, PACK * HALF], F32, name="wa_raw%d" % h, offset=4096 * h)
+            wa_raw.append(raw[:].rearrange("p (j c) -> p j c", j=PACK))
+            nc.sync.dma_start(wa_raw[h], wa_rows[:, :, h * HALF : (h + 1) * HALF])
 
         gw = sb("gw", [P, S], U32, tag="bytes_then_words")
         dw = sb("dw", [P, S], U32)
         nc.vector.tensor_copy(gw[:], xw[:].indirect(offs_t[:]))
         nc.vector.tensor_copy(
-            dw[:].bitcast(I32).rearrange("p (s m) -> p m s", s=PACK),
-            gw[:].bitcast(I32).rearrange("p (m s) -> p m s", s=PACK),
+            dw[:].bitcast(I32).rearrange("p (s c i) -> p c s i", s=PACK, i=4),
+            gw[:].bitcast(I32).rearrange("p (c i s) -> p c s i", s=PACK, i=4),
         )
 
         def project(codes, scales, c):
@@ -107,8 +111,9 @@ def tile_picked_selmom_none_po_kernel(
 
         wb_bf = [
             sb("wb_bf0", [P, P * PACK], BF16),
-            sb("wb_bf1", [P, P * PACK], BF16, tag="bytes_then_words"),
-            sb("wb_bf2", [P, HALF * PACK], BF16),
+            sb("wb_bf1", [P, P * PACK], BF16),
+            sb("wb_bf2", [P, P * PACK], BF16, tag="bytes_then_words"),
+            sb("wb_bf3", [P, P * PACK], BF16),
         ]
         wb_c = sb("wb_c", [P, N], U32, tag="words_then_codes")
         wb_s = sb("wb_s", [P, N], U8)
@@ -133,17 +138,15 @@ def tile_picked_selmom_none_po_kernel(
             weigh(z2_bf[:, c * P * PACK : (c + 1) * P * PACK].rearrange("p (m s) -> p m s", s=PACK), acc, gi_t)
 
         weave(nc.scalar.copy, wb_bf[0], 0, P)
-        weave(nc.vector.tensor_copy, wb_bf[1], P, HALF)
+        weave(nc.scalar.copy, wb_bf[1], P, 2 * P)
+        weave(nc.scalar.copy, wb_bf[3], 3 * P, 4 * P)
         quant(wb_c, wb_s, wb_bf[0][:], 0, P)
-        quant(wb_c, wb_s, wb_bf[1][:], P, HALF)
-        weave(nc.scalar.copy, wb_bf[2], HALF, N)
-        second(0)
-        second(1)
-        quant(wb_c, wb_s, wb_bf[2][:], HALF, N)
-        quant(z2_c, z2_s, z2_bf[:, 0 : HALF * PACK], 0, HALF)
-        second(2)
-        second(3)
-        quant(z2_c, z2_s, z2_bf[:, HALF * PACK : N * PACK], HALF, N)
+        quant(wb_c, wb_s, wb_bf[1][:], P, 2 * P)
+        weave(nc.vector.tensor_copy, wb_bf[2], 2 * P, 3 * P)
+        quant(wb_c, wb_s, wb_bf[3][:], 3 * P, 4 * P)
+        quant(wb_c, wb_s, wb_bf[2][:], 2 * P, 3 * P)
+        for c in (0, 1, 3, 2):
+            second(c)
 
         wa_bf = sb("wa_bf", [P, H * PACK], BF16)
         wa_c = sb("wa_c", [P, H], U32)
@@ -153,17 +156,34 @@ def tile_picked_selmom_none_po_kernel(
             nc.scalar.copy(
                 wa_view[:, h * 64 : (h + 1) * 64, :, :], wa_raw[h].rearrange("p j (m t) -> p m j t", t=PACK)
             )
-        z_bf = sb("z_bf", [P, H * PACK], BF16)
+        z_bf = sb("z_bf", [P, HALF * PACK], BF16)
+        z_hi = sb("z_hi", [P, HALF * PACK], BF16, tag="factor_then_result")
         z_c = sb("z_c", [P, H], U32)
         z_s = sb("z_s", [P, H], U8)
-        y = sb("y", [P, PACK, V], F32)
         out_rows = out_0.rearrange("(p t) v -> p t v", t=PACK)
-        accs = []
-        for t in range(PACK):
-            part = slice(t * P * PACK, (t + 1) * P * PACK)
-            colr = slice(t * P, (t + 1) * P)
-            nc.vector.quantize_mx(out=wa_c[:, colr].bitcast(FP8X4), scales=wa_s[:, colr], in_=wa_bf[:, part])
-            accs.append(project(wa_c, wa_s, ("late", t)))
+        quant(wa_c, wa_s, wa_bf[:, 0 : P * PACK], 0, P)
+        quant(wa_c, wa_s, wa_bf[:, HALF * PACK : H * PACK], HALF, H)
+        quant(wa_c, wa_s, wa_bf[:, P * PACK : HALF * PACK], P, HALF)
+        quant(z2_c, z2_s, z2_bf[:], 0, N)
+        accs = [project(wa_c, wa_s, ("late", 0))]
+        planes = sb("planes", [P, PACK * HALF], BF16)
+        for u in range(2):
+            acc = psum.tile([P, 2, HALF], F32, name="late")
+            for s in (2 * u, 2 * u + 1):
+                nc.tensor.matmul_mx(
+                    out=acc[:, s - 2 * u, :],
+                    lhsT=dw[:, s * P : (s + 1) * P].bitcast(FP8X4),
+                    lhsT_scale=ds[:, s * P : (s + 1) * P],
+                    rhs=wa_c[:, HALF:H].bitcast(FP8X4),
+                    rhs_scale=wa_s[:, HALF:H],
+                    start=True,
+                    stop=True,
+                )
+            for s in (2 * u, 2 * u + 1):
+                nc.scalar.activation(
+                    planes[:, s * HALF : (s + 1) * HALF], acc[:, s - 2 * u, :], COPY, scale=gt_t[:, s : s + 1]
+                )
+        accs.append(project(wa_c, wa_s, ("late", 1)))
         wins = []
 
         def first(t):
@@ -171,7 +191,6 @@ def tile_picked_selmom_none_po_kernel(
 
         def moments(t):
             colr = slice(t * P, (t + 1) * P)
-            quant(z_c, z_s, z_bf[:, t * P * PACK : (t + 1) * P * PACK], t * P, (t + 1) * P)
             cv = psum.tile([P, N], F32, name="early")
             nc.tensor.matmul_mx(
                 out=cv[:],
@@ -186,17 +205,24 @@ def tile_picked_selmom_none_po_kernel(
             nc.scalar.activation(win[:], cv[:], TANH, bias=bias[:], scale=0.0625)
             wins.append(win)
 
+        first(0)
+        quant(z_c, z_s, z_bf[:, 0 : P * PACK], 0, P)
+        first(1)
+        nc.vector.tensor_copy(
+            z_hi[:].rearrange("p (c i s) -> p c s i", i=4, s=PACK),
+            planes[:].rearrange("p (s c i) -> p c s i", s=PACK, i=4),
+        )
+        quant(z_c, z_s, z_bf[:, P * PACK : HALF * PACK], P, HALF)
+        quant(z_c, z_s, z_hi[:], HALF, H)
+        y = sb("y", [P, PACK, V], F32, tag="factor_then_result")
+        for t in range(PACK):
+            moments(t)
+
         def fetch(t):
             nc.vector.tensor_copy(y[:, t, :], wins[t][:].indirect(cols_t[:]))
             nc.sync.dma_start(out_rows[:, t, :], y[:, t, :])
 
-        first(0)
-        for t in range(1, PACK):
-            first(t)
-            moments(t - 1)
-        fetch(0)
-        moments(PACK - 1)
-        for t in range(1, PACK):
+        for t in range(PACK):
             fetch(t)
 
         y_bf = sb("y_bf", [P, V * PACK], BF16)

@@ -117,7 +117,9 @@ def tile_picked_selmom_none_po_kernel(
         ]
         wb_c = sb("wb_c", [P, N], U32, tag="words_then_codes")
         wb_s = sb("wb_s", [P, N], U8)
-        z2_bf = sb("z2_bf", [P, N * PACK], BF16)
+        z2_lo = sb("z2_lo", [P, HALF * PACK], BF16)
+        z2_part = {0: z2_lo[:, 0 : P * PACK], 1: z2_lo[:, P * PACK : HALF * PACK]}
+        z2_part[3] = sb("z2_3", [P, P * PACK], BF16)[:]
         z2_c = sb("z2_c", [P, N], U32)
         z2_s = sb("z2_s", [P, N], U8)
 
@@ -134,8 +136,7 @@ def tile_picked_selmom_none_po_kernel(
             )
 
         def second(c):
-            acc = project(wb_c, wb_s, ("early", c))
-            weigh(z2_bf[:, c * P * PACK : (c + 1) * P * PACK].rearrange("p (m s) -> p m s", s=PACK), acc, gi_t)
+            weigh(z2_part[c].rearrange("p (m s) -> p m s", s=PACK), b_acc[c], gi_t)
 
         weave(nc.scalar.copy, wb_bf[0], 0, P)
         weave(nc.scalar.copy, wb_bf[1], P, 2 * P)
@@ -145,17 +146,21 @@ def tile_picked_selmom_none_po_kernel(
         weave(nc.vector.tensor_copy, wb_bf[2], 2 * P, 3 * P)
         quant(wb_c, wb_s, wb_bf[3][:], 3 * P, 4 * P)
         quant(wb_c, wb_s, wb_bf[2][:], 2 * P, 3 * P)
+        b_acc = {}
         for c in (0, 1, 3, 2):
-            second(c)
+            b_acc[c] = project(wb_c, wb_s, ("early", c))
+        second(0)
 
-        wa_bf = sb("wa_bf", [P, H * PACK], BF16)
+        wa_bf = sb("wa_bf", [P, H * PACK], BF16, tag="weights_then_factor")
         wa_c = sb("wa_c", [P, H], U32)
         wa_s = sb("wa_s", [P, H], U8)
         wa_view = wa_bf[:].rearrange("p (t m j) -> p m j t", t=PACK, j=PACK)
-        for h in range(2):
-            nc.scalar.copy(
-                wa_view[:, h * 64 : (h + 1) * 64, :, :], wa_raw[h].rearrange("p j (m t) -> p m j t", t=PACK)
-            )
+        wa_src = [raw.rearrange("p j (m t) -> p m j t", t=PACK) for raw in wa_raw]
+        nc.scalar.copy(wa_view[:, 0:64], wa_src[0])
+        nc.scalar.copy(wa_view[:, 64:96], wa_src[1][:, 0:32])
+        nc.vector.tensor_copy(wa_view[:, 96:128], wa_src[1][:, 32:64])
+        second(1)
+        second(3)
         z_bf = sb("z_bf", [P, HALF * PACK], BF16)
         z_hi = sb("z_hi", [P, HALF * PACK], BF16, tag="factor_then_result")
         z_c = sb("z_c", [P, H], U32)
@@ -164,7 +169,10 @@ def tile_picked_selmom_none_po_kernel(
         quant(wa_c, wa_s, wa_bf[:, 0 : P * PACK], 0, P)
         quant(wa_c, wa_s, wa_bf[:, HALF * PACK : H * PACK], HALF, H)
         quant(wa_c, wa_s, wa_bf[:, P * PACK : HALF * PACK], P, HALF)
-        quant(z2_c, z2_s, z2_bf[:], 0, N)
+        quant(z2_c, z2_s, z2_lo[:], 0, HALF)
+        quant(z2_c, z2_s, z2_part[3], 3 * P, 4 * P)
+        z2_part[2] = sb("z2_2", [P, P * PACK], BF16, tag="weights_then_factor")[:]
+        second(2)
         accs = [project(wa_c, wa_s, ("late", 0))]
         planes = sb("planes", [P, PACK * HALF], BF16)
         for u in range(2):
@@ -206,6 +214,7 @@ def tile_picked_selmom_none_po_kernel(
             wins.append(win)
 
         first(0)
+        quant(z2_c, z2_s, z2_part[2], 2 * P, 3 * P)
         quant(z_c, z_s, z_bf[:, 0 : P * PACK], 0, P)
         first(1)
         nc.vector.tensor_copy(
@@ -222,17 +231,23 @@ def tile_picked_selmom_none_po_kernel(
             nc.vector.tensor_copy(y[:, t, :], wins[t][:].indirect(cols_t[:]))
             nc.sync.dma_start(out_rows[:, t, :], y[:, t, :])
 
-        for t in range(PACK):
+        for t in range(PACK - 1):
             fetch(t)
+        last = PACK - 1
+        for h in range(2):
+            nc.vector.tensor_copy(y[:, last, h * P : (h + 1) * P], wins[last][:].indirect(cols_t[:, 8 * h : 8 * h + 8]))
+        nc.sync.dma_start(out_rows[:, last, :], y[:, last, :])
 
         y_bf = sb("y_bf", [P, V * PACK], BF16)
         y_c = sb("y_c", [P, V], U32)
         y_s = sb("y_s", [P, V], U8)
-        y_dst = y_bf[:].rearrange("p (c i t) -> p c t i", i=4, t=PACK)
-        y_src = y[:].rearrange("p t (c i) -> p c t i", i=4)
-        nc.vector.tensor_copy(y_dst[:, 0:44], y_src[:, 0:44])
-        nc.scalar.copy(y_dst[:, 44:64], y_src[:, 44:64])
-        nc.vector.quantize_mx(out=y_c[:].bitcast(FP8X4), scales=y_s[:], in_=y_bf[:])
+        y_dst = y_bf[:].rearrange("p (c t) -> p c t", t=PACK)
+        y_src = y[:].rearrange("p t c -> p c t")
+        nc.scalar.copy(y_dst[:, :, 0:2], y_src[:, :, 0:2])
+        for h in range(2):
+            nc.vector.tensor_copy(y_dst[:, h * P : (h + 1) * P, 2:4], y_src[:, h * P : (h + 1) * P, 2:4])
+        for h in range(2):
+            quant(y_c, y_s, y_bf[:, h * P * PACK : (h + 1) * P * PACK], h * P, (h + 1) * P)
         nc.sync.dma_start(out_1[0].rearrange("p c r -> p (c r)").bitcast(I32), y_c[:].bitcast(I32))
         for q in range(4):
             eng = nc.scalar if q % 2 == 0 else nc.sync

@@ -28,7 +28,7 @@ def tile_picked_selmom_none_po_kernel(
     with ExitStack() as ctx:
         keep = ctx.enter_context(tc.tile_pool(name="keep", bufs=1))
         shared = ctx.enter_context(tc.tile_pool(name="shared", bufs=1))
-        psum = ctx.enter_context(tc.psum_pool(name="psum", bufs=4))
+        psum = ctx.enter_context(tc.psum_pool(name="psum", bufs=1))
 
         def sb(name, shape, dtype, tag=None):
             return keep.tile(shape, dtype, name=name, tag=tag or name, align_bytes=64)
@@ -135,6 +135,18 @@ def tile_picked_selmom_none_po_kernel(
                 out=codes[:, lo:hi].bitcast(FP8X4), scales=scales[:, lo:hi], in_=src
             )
 
+        def keep_warm(bank):
+            spare = psum.tile([P, N], F32, name=bank)
+            nc.tensor.matmul_mx(
+                out=spare[:],
+                lhsT=dw[:, 0:P].bitcast(FP8X4),
+                lhsT_scale=ds[:, 0:P],
+                rhs=wb_c[:].bitcast(FP8X4),
+                rhs_scale=wb_s[:],
+                start=True,
+                stop=True,
+            )
+
         def second(c):
             weigh(z2_part[c].rearrange("p (m s) -> p m s", s=PACK), b_acc[c], gi_t)
 
@@ -148,7 +160,7 @@ def tile_picked_selmom_none_po_kernel(
         quant(wb_c, wb_s, wb_bf[2][:], 2 * P, 3 * P)
         b_acc = {}
         for c in (0, 1, 3, 2):
-            b_acc[c] = project(wb_c, wb_s, ("early", c))
+            b_acc[c] = project(wb_c, wb_s, ("bank_b%d" % c, c))
         second(0)
 
         wa_bf = sb("wa_bf", [P, H * PACK], BF16, tag="weights_then_factor")
@@ -160,6 +172,7 @@ def tile_picked_selmom_none_po_kernel(
         nc.scalar.copy(wa_view[:, 64:96], wa_src[1][:, 0:32])
         nc.vector.tensor_copy(wa_view[:, 96:128], wa_src[1][:, 32:64])
         second(1)
+        keep_warm("bank_b1")
         second(3)
         z_bf = sb("z_bf", [P, HALF * PACK], BF16)
         z_hi = sb("z_hi", [P, HALF * PACK], BF16, tag="factor_then_result")
@@ -173,10 +186,10 @@ def tile_picked_selmom_none_po_kernel(
         quant(z2_c, z2_s, z2_part[3], 3 * P, 4 * P)
         z2_part[2] = sb("z2_2", [P, P * PACK], BF16, tag="weights_then_factor")[:]
         second(2)
-        accs = [project(wa_c, wa_s, ("late", 0))]
+        accs = [project(wa_c, wa_s, ("bank_a0", 0))]
         planes = sb("planes", [P, PACK * HALF], BF16)
         for u in range(2):
-            acc = psum.tile([P, 2, HALF], F32, name="late")
+            acc = psum.tile([P, 2, HALF], F32, name="bank_u%d" % u)
             for s in (2 * u, 2 * u + 1):
                 nc.tensor.matmul_mx(
                     out=acc[:, s - 2 * u, :],
@@ -191,7 +204,7 @@ def tile_picked_selmom_none_po_kernel(
                 nc.scalar.activation(
                     planes[:, s * HALF : (s + 1) * HALF], acc[:, s - 2 * u, :], COPY, scale=gt_t[:, s : s + 1]
                 )
-        accs.append(project(wa_c, wa_s, ("late", 1)))
+        accs.append(project(wa_c, wa_s, ("bank_a1", 1)))
         wins = []
 
         def first(t):
@@ -199,7 +212,7 @@ def tile_picked_selmom_none_po_kernel(
 
         def moments(t):
             colr = slice(t * P, (t + 1) * P)
-            cv = psum.tile([P, N], F32, name="early")
+            cv = psum.tile([P, N], F32, name="bank_b%d" % (0, 1, 3, 2)[t])
             nc.tensor.matmul_mx(
                 out=cv[:],
                 lhsT=z_c[:, colr].bitcast(FP8X4),
@@ -214,9 +227,11 @@ def tile_picked_selmom_none_po_kernel(
             wins.append(win)
 
         first(0)
+        keep_warm("bank_a0")
         quant(z2_c, z2_s, z2_part[2], 2 * P, 3 * P)
         quant(z_c, z_s, z_bf[:, 0 : P * PACK], 0, P)
         first(1)
+        keep_warm("bank_a1")
         nc.vector.tensor_copy(
             z_hi[:].rearrange("p (c i s) -> p c s i", i=4, s=PACK),
             planes[:].rearrange("p (s c i) -> p c s i", s=PACK, i=4),

@@ -19,6 +19,7 @@ MULT = mybir.AluOpType.mult
 P = 128
 PACK = 4
 HALF = 256
+QUARTER = P * PACK
 
 
 def tile_picked_selmom_none_po_kernel(
@@ -33,236 +34,221 @@ def tile_picked_selmom_none_po_kernel(
         def sb(name, shape, dtype, tag=None):
             return keep.tile(shape, dtype, name=name, tag=tag or name, align_bytes=64)
 
+        def quant(codes, scales, src, lo, hi):
+            nc.vector.quantize_mx(out=codes[:, lo:hi].bitcast(FP8X4), scales=scales[:, lo:hi], in_=src)
+
+        def product(out, lhs_c, lhs_s, lhs_cols, rhs_c, rhs_s, rhs_cols):
+            nc.tensor.matmul_mx(
+                out=out,
+                lhsT=lhs_c[:, lhs_cols].bitcast(FP8X4),
+                lhsT_scale=lhs_s[:, lhs_cols],
+                rhs=rhs_c[:, rhs_cols].bitcast(FP8X4),
+                rhs_scale=rhs_s[:, rhs_cols],
+                start=True,
+                stop=True,
+            )
+
+        def block(i, width=P):
+            return slice(i * width, (i + 1) * width)
+
         offs_t = sb("offs_t", [P, S // 16], U16)
         cols_t = sb("cols_t", [P, V // 16], U16)
-        nc.sync.dma_start(offs_t[:], offs)
+        gt_t = sb("gt_t", [P, PACK], F32)
+        gi_t = sb("gi_t", [P, PACK], F32)
         xs = sb("xs", [P, T], U8, tag="bytes_then_words")
+        xw = sb("xw", [P, T], U32, tag="words_then_codes")
         nc.sync.dma_start(
             xs[:].bitcast(I32),
             x_scales[0].bitcast(I32).rearrange("q (o c) -> q o c", o=1).broadcast_to([16, 8, T // 4]),
         )
-        nc.sync.dma_start(cols_t[:], cols)
-
-        gt_t = sb("gt_t", [P, PACK], F32)
-        gi_t = sb("gi_t", [P, PACK], F32)
+        nc.sync.dma_start(offs_t[:], offs)
+        nc.sync.dma_start(xw[:].bitcast(I32), x_words[0].rearrange("p c r -> p (c r)").bitcast(I32))
         nc.scalar.dma_start(gi_t[:], gi.rearrange("(p s) o -> p (s o)", s=PACK))
         nc.scalar.dma_start(gt_t[:], gt.rearrange("(p s) o -> p (s o)", s=PACK))
 
         zero = sb("zero", [P, 1], F32)
-        bias = sb("bias", [P, 1], F32)
+        bias = sb("bias", [P, 1], F32, tag="bias_then_rounded")
         nc.vector.memset(zero[:], 0.0)
         nc.scalar.activation(bias[:], zero[:], TANH)
 
-        xw = sb("xw", [P, T], U32, tag="words_then_codes")
-        nc.sync.dma_start(xw[:].bitcast(I32), x_words[0].rearrange("p c r -> p (c r)").bitcast(I32))
-
         wb_rows = wb.rearrange("(p j) c -> p j c", j=PACK)
         wa_rows = wa.rearrange("(p j) c -> p j c", j=PACK)
-        wb_raw = []
-        for h in range(2):
-            raw = sb("wb_raw%d" % h, [P, PACK * HALF], F32)
-            wb_raw.append(raw[:].rearrange("p (j c) -> p j c", j=PACK))
-            nc.sync.dma_start(wb_raw[h], wb_rows[:, :, h * HALF : (h + 1) * HALF])
 
-        gs = shared.tile([P, S], U8, name="gs", offset=4096 - S // 2)
+        def by_row(flat):
+            return flat.rearrange("p (j c) -> p j c", j=PACK)
+
+        wb_lo = by_row(sb("wb_lo", [P, QUARTER], F32)[:])
+        wb_mid = by_row(sb("wb_mid", [P, 2 * QUARTER], F32)[:])
+        nc.sync.dma_start(wb_lo, wb_rows[:, :, block(0)])
+        nc.sync.dma_start(wb_mid, wb_rows[:, :, P : 3 * P])
+        nc.sync.dma_start(cols_t[:], cols)
+
+        gs_room = shared.tile([P, 5 * QUARTER * 4], U8, name="gs_room", offset=0)
+        gs = [gs_room[:, block(h, HALF)] for h in range(2)]
         ds = sb("ds", [P, S], U8)
-        nc.vector.tensor_copy(gs[:], xs[:].indirect(offs_t[:]))
-        nc.vector.tensor_copy(
-            ds[:].rearrange("p (s c i) -> p c s i", s=PACK, i=16), gs[:].rearrange("p (c i s) -> p c s i", s=PACK, i=16)
-        )
+        for h in range(2):
+            nc.vector.tensor_copy(gs[h], xs[:].indirect(offs_t[:, block(h, 16)]))
+        for h in range(2):
+            nc.vector.tensor_copy(
+                ds[:].rearrange("p (s c i) -> p c s i", s=PACK, i=16)[:, block(h, 4)],
+                gs[h].rearrange("p (c i s) -> p c s i", s=PACK, i=16),
+            )
         for a in range(1, 4):
             nc.sync.dma_start(ds[a:P:32, :].bitcast(I32), ds[8 * a : P : 32, :].bitcast(I32))
 
-        wa_raw = []
+        wb_hi = by_row(shared.tile([P, QUARTER], F32, name="wb_hi", offset=0)[:])
+        wa_raw = [
+            by_row(shared.tile([P, 2 * QUARTER], F32, name="wa_raw%d" % h, offset=(1 + 2 * h) * QUARTER * 4)[:])
+            for h in range(2)
+        ]
+        nc.sync.dma_start(wb_hi, wb_rows[:, :, block(3)])
         for h in range(2):
-            raw = shared.tile([P, PACK * HALF], F32, name="wa_raw%d" % h, offset=4096 * h)
-            wa_raw.append(raw[:].rearrange("p (j c) -> p j c", j=PACK))
-            nc.sync.dma_start(wa_raw[h], wa_rows[:, :, h * HALF : (h + 1) * HALF])
+            nc.sync.dma_start(wa_raw[h], wa_rows[:, :, block(h, HALF)])
+        wb_raw = [wb_lo, wb_mid[:, :, block(0)], wb_mid[:, :, block(1)], wb_hi]
 
         gw = sb("gw", [P, S], U32, tag="bytes_then_words")
         dw = sb("dw", [P, S], U32)
         nc.vector.tensor_copy(gw[:], xw[:].indirect(offs_t[:]))
-        nc.vector.tensor_copy(
-            dw[:].bitcast(I32).rearrange("p (s c i) -> p c s i", s=PACK, i=4),
-            gw[:].bitcast(I32).rearrange("p (c i s) -> p c s i", s=PACK, i=4),
-        )
 
-        def project(codes, scales, c):
-            acc = psum.tile([P, PACK, P], F32, name=c[0])
+        wb_bf = [sb("wb_bf%d" % c, [P, QUARTER], BF16) for c in range(4)]
+        wb_c = sb("wb_c", [P, N], U32, tag="words_then_codes")
+        wb_s = sb("wb_s", [P, N], U8)
+        z2_bf = sb("z2_bf", [P, N * PACK], BF16)
+
+        def weave_b(eng, c):
+            eng(
+                wb_bf[c][:].rearrange("p (c i j) -> p c j i", i=4, j=PACK),
+                wb_raw[c].rearrange("p j (c i) -> p c j i", i=4),
+            )
+
+        def quant_b(c):
+            quant(wb_c, wb_s, wb_bf[c][:], c * P, (c + 1) * P)
+
+        def project_b(c):
+            b_acc.append(project("bank_b%d" % c, wb_c, wb_s, c))
+
+        def project(name, codes, scales, c):
+            acc = psum.tile([P, PACK, P], F32, name=name)
             for s in range(PACK):
-                nc.tensor.matmul_mx(
-                    out=acc[:, s, :],
-                    lhsT=dw[:, s * P : (s + 1) * P].bitcast(FP8X4),
-                    lhsT_scale=ds[:, s * P : (s + 1) * P],
-                    rhs=codes[:, c[1] * P : (c[1] + 1) * P].bitcast(FP8X4),
-                    rhs_scale=scales[:, c[1] * P : (c[1] + 1) * P],
-                    start=True,
-                    stop=True,
-                )
+                product(acc[:, s, :], dw, ds, block(s), codes, scales, block(c))
             return acc
 
         def weigh(dst, acc, gate):
             nc.vector.tensor_tensor(
-                dst,
+                dst.rearrange("p (m s) -> p m s", s=PACK),
                 acc[:].rearrange("p s m -> p m s"),
                 gate[:].rearrange("p (o s) -> p o s", o=1).broadcast_to([P, P, PACK]),
                 MULT,
             )
 
-        wb_bf = [
-            sb("wb_bf0", [P, P * PACK], BF16),
-            sb("wb_bf1", [P, P * PACK], BF16),
-            sb("wb_bf2", [P, P * PACK], BF16, tag="bytes_then_words"),
-            sb("wb_bf3", [P, P * PACK], BF16),
-        ]
-        wb_c = sb("wb_c", [P, N], U32, tag="words_then_codes")
-        wb_s = sb("wb_s", [P, N], U8)
-        z2_lo = sb("z2_lo", [P, HALF * PACK], BF16)
-        z2_part = {0: z2_lo[:, 0 : P * PACK], 1: z2_lo[:, P * PACK : HALF * PACK]}
-        z2_part[3] = sb("z2_3", [P, P * PACK], BF16)[:]
-        z2_c = sb("z2_c", [P, N], U32)
-        z2_s = sb("z2_s", [P, N], U8)
-
-        def weave(eng, dst, lo, hi):
-            h = lo // HALF
-            eng(
-                dst[:].rearrange("p (c i j) -> p c j i", i=4, j=PACK),
-                wb_raw[h][:, :, lo - h * HALF : hi - h * HALF].rearrange("p j (c i) -> p c j i", i=4),
-            )
-
-        def quant(codes, scales, src, lo, hi):
-            nc.vector.quantize_mx(
-                out=codes[:, lo:hi].bitcast(FP8X4), scales=scales[:, lo:hi], in_=src
-            )
-
         def keep_warm(bank):
             spare = psum.tile([P, N], F32, name=bank)
-            nc.tensor.matmul_mx(
-                out=spare[:],
-                lhsT=dw[:, 0:P].bitcast(FP8X4),
-                lhsT_scale=ds[:, 0:P],
-                rhs=wb_c[:].bitcast(FP8X4),
-                rhs_scale=wb_s[:],
-                start=True,
-                stop=True,
+            product(spare[:], dw, ds, block(0), wb_c, wb_s, slice(0, N))
+
+        b_acc = []
+        weave_b(nc.scalar.copy, 0)
+        weave_b(nc.scalar.copy, 1)
+        weave_b(nc.scalar.copy, 3)
+        quant_b(0)
+        for u in range(2):
+            nc.vector.tensor_copy(
+                dw[:].bitcast(I32).rearrange("p (s c i) -> p c s i", s=PACK, i=4)[:, :, block(u, 2)],
+                gw[:].bitcast(I32).rearrange("p (c i s) -> p c s i", s=PACK, i=4)[:, :, block(u, 2)],
             )
+        project_b(0)
+        weave_b(nc.vector.tensor_copy, 2)
+        for c in (1, 2):
+            quant_b(c)
+            project_b(c)
+        weigh(z2_bf[:, block(0, QUARTER)], b_acc[0], gi_t)
+        quant_b(3)
+        project_b(3)
+        weigh(z2_bf[:, block(1, QUARTER)], b_acc[1], gi_t)
+        keep_warm("bank_b1")
 
-        def second(c):
-            weigh(z2_part[c].rearrange("p (m s) -> p m s", s=PACK), b_acc[c], gi_t)
-
-        weave(nc.scalar.copy, wb_bf[0], 0, P)
-        weave(nc.scalar.copy, wb_bf[1], P, 2 * P)
-        weave(nc.scalar.copy, wb_bf[3], 3 * P, 4 * P)
-        quant(wb_c, wb_s, wb_bf[0][:], 0, P)
-        quant(wb_c, wb_s, wb_bf[1][:], P, 2 * P)
-        weave(nc.vector.tensor_copy, wb_bf[2], 2 * P, 3 * P)
-        quant(wb_c, wb_s, wb_bf[3][:], 3 * P, 4 * P)
-        quant(wb_c, wb_s, wb_bf[2][:], 2 * P, 3 * P)
-        b_acc = {}
-        for c in (0, 1, 3, 2):
-            b_acc[c] = project(wb_c, wb_s, ("bank_b%d" % c, c))
-        second(0)
-
-        wa_bf = sb("wa_bf", [P, H * PACK], BF16, tag="weights_then_factor")
+        wa_bf = sb("wa_bf", [P, H * PACK], BF16, tag="weights_then_codes")
         wa_c = sb("wa_c", [P, H], U32)
         wa_s = sb("wa_s", [P, H], U8)
         wa_view = wa_bf[:].rearrange("p (t m j) -> p m j t", t=PACK, j=PACK)
         wa_src = [raw.rearrange("p j (m t) -> p m j t", t=PACK) for raw in wa_raw]
         nc.scalar.copy(wa_view[:, 0:64], wa_src[0])
-        nc.scalar.copy(wa_view[:, 64:96], wa_src[1][:, 0:32])
-        nc.vector.tensor_copy(wa_view[:, 96:128], wa_src[1][:, 32:64])
-        second(1)
-        keep_warm("bank_b1")
-        second(3)
-        z_bf = sb("z_bf", [P, HALF * PACK], BF16)
+        weigh(z2_bf[:, block(2, QUARTER)], b_acc[2], gi_t)
+        keep_warm("bank_b2")
+        z2_s = [sb("z2_s%d" % h, [P, HALF], U8) for h in range(2)]
+        z2_c = [sb("z2_c0", [P, HALF], U32)]
+        quant(z2_c[0], z2_s[0], z2_bf[:, block(0, 2 * QUARTER)], 0, HALF)
+        weigh(z2_bf[:, block(3, QUARTER)], b_acc[3], gi_t)
+        keep_warm("bank_b3")
+        nc.scalar.copy(wa_view[:, 64:128], wa_src[1])
+        quant(wa_c, wa_s, wa_bf[:, block(0, QUARTER)], 0, P)
+        quant(wa_c, wa_s, wa_bf[:, block(1, 2 * QUARTER)], HALF, H)
+        quant(wa_c, wa_s, wa_bf[:, block(1, QUARTER)], P, HALF)
+        z2_c.append(sb("z2_c1", [P, HALF], U32, tag="weights_then_codes"))
+        quant(z2_c[1], z2_s[1], z2_bf[:, block(1, 2 * QUARTER)], 0, HALF)
+
+        z_lo = sb("z_lo", [P, HALF * PACK], BF16)
         z_hi = sb("z_hi", [P, HALF * PACK], BF16, tag="factor_then_result")
         z_c = sb("z_c", [P, H], U32)
         z_s = sb("z_s", [P, H], U8)
-        out_rows = out_0.rearrange("(p t) v -> p t v", t=PACK)
-        quant(wa_c, wa_s, wa_bf[:, 0 : P * PACK], 0, P)
-        quant(wa_c, wa_s, wa_bf[:, HALF * PACK : H * PACK], HALF, H)
-        quant(wa_c, wa_s, wa_bf[:, P * PACK : HALF * PACK], P, HALF)
-        quant(z2_c, z2_s, z2_lo[:], 0, HALF)
-        quant(z2_c, z2_s, z2_part[3], 3 * P, 4 * P)
-        z2_part[2] = sb("z2_2", [P, P * PACK], BF16, tag="weights_then_factor")[:]
-        second(2)
-        accs = [project(wa_c, wa_s, ("bank_a0", 0))]
-        planes = sb("planes", [P, PACK * HALF], BF16)
+        planes = sb("planes", [P, PACK, HALF], BF16)
+        a_acc = []
         for u in range(2):
+            a_acc.append(project("bank_a%d" % u, wa_c, wa_s, u))
             acc = psum.tile([P, 2, HALF], F32, name="bank_u%d" % u)
             for s in (2 * u, 2 * u + 1):
-                nc.tensor.matmul_mx(
-                    out=acc[:, s - 2 * u, :],
-                    lhsT=dw[:, s * P : (s + 1) * P].bitcast(FP8X4),
-                    lhsT_scale=ds[:, s * P : (s + 1) * P],
-                    rhs=wa_c[:, HALF:H].bitcast(FP8X4),
-                    rhs_scale=wa_s[:, HALF:H],
-                    start=True,
-                    stop=True,
-                )
+                product(acc[:, s - 2 * u, :], dw, ds, block(s), wa_c, wa_s, slice(HALF, H))
             for s in (2 * u, 2 * u + 1):
-                nc.scalar.activation(
-                    planes[:, s * HALF : (s + 1) * HALF], acc[:, s - 2 * u, :], COPY, scale=gt_t[:, s : s + 1]
-                )
-        accs.append(project(wa_c, wa_s, ("bank_a1", 1)))
+                nc.scalar.activation(planes[:, s, :], acc[:, s - 2 * u, :], COPY, scale=gt_t[:, s : s + 1])
+
         wins = []
 
-        def first(t):
-            weigh(z_bf[:, t * P * PACK : (t + 1) * P * PACK].rearrange("p (m s) -> p m s", s=PACK), accs[t], gt_t)
-
         def moments(t):
-            colr = slice(t * P, (t + 1) * P)
-            cv = psum.tile([P, N], F32, name="bank_b%d" % (0, 1, 3, 2)[t])
-            nc.tensor.matmul_mx(
-                out=cv[:],
-                lhsT=z_c[:, colr].bitcast(FP8X4),
-                lhsT_scale=z_s[:, colr],
-                rhs=z2_c[:].bitcast(FP8X4),
-                rhs_scale=z2_s[:],
-                start=True,
-                stop=True,
-            )
+            cv = psum.tile([P, N], F32, name="bank_b%d" % t)
+            for h in range(2):
+                product(cv[:, block(h, HALF)], z_c, z_s, block(t), z2_c[h], z2_s[h], slice(0, HALF))
             win = sb("win%d" % t, [P, N], F32)
             nc.scalar.activation(win[:], cv[:], TANH, bias=bias[:], scale=0.0625)
             wins.append(win)
 
-        first(0)
-        keep_warm("bank_a0")
-        quant(z2_c, z2_s, z2_part[2], 2 * P, 3 * P)
-        quant(z_c, z_s, z_bf[:, 0 : P * PACK], 0, P)
-        first(1)
-        keep_warm("bank_a1")
-        nc.vector.tensor_copy(
-            z_hi[:].rearrange("p (c i s) -> p c s i", i=4, s=PACK),
-            planes[:].rearrange("p (s c i) -> p c s i", s=PACK, i=4),
-        )
-        quant(z_c, z_s, z_bf[:, P * PACK : HALF * PACK], P, HALF)
-        quant(z_c, z_s, z_hi[:], HALF, H)
-        y = sb("y", [P, PACK, V], F32, tag="factor_then_result")
-        for t in range(PACK):
-            moments(t)
+        def interleave(eng, u):
+            eng(
+                z_hi[:, block(u, QUARTER)].rearrange("p (c i s) -> p c s i", i=4, s=PACK),
+                planes[:, :, block(u)].rearrange("p s (c i) -> p c s i", i=4),
+            )
 
-        def fetch(t):
+        weigh(z_lo[:, block(0, QUARTER)], a_acc[0], gt_t)
+        weigh(z_lo[:, block(1, QUARTER)], a_acc[1], gt_t)
+        quant(z_c, z_s, z_lo[:, block(0, QUARTER)], 0, P)
+        moments(0)
+        interleave(nc.vector.tensor_copy, 0)
+        quant(z_c, z_s, z_lo[:, block(1, QUARTER)], P, HALF)
+        moments(1)
+        interleave(nc.vector.tensor_copy, 1)
+        quant(z_c, z_s, z_hi[:, block(0, QUARTER)], HALF, HALF + P)
+        moments(2)
+        quant(z_c, z_s, z_hi[:, block(1, QUARTER)], HALF + P, H)
+        moments(3)
+
+        y = sb("y", [P, PACK, V], F32, tag="factor_then_result")
+        out_rows = out_0.rearrange("(p t) v -> p t v", t=PACK)
+        last = PACK - 1
+        for t in range(last):
             nc.vector.tensor_copy(y[:, t, :], wins[t][:].indirect(cols_t[:]))
             nc.sync.dma_start(out_rows[:, t, :], y[:, t, :])
-
-        for t in range(PACK - 1):
-            fetch(t)
-        last = PACK - 1
         for h in range(2):
-            nc.vector.tensor_copy(y[:, last, h * P : (h + 1) * P], wins[last][:].indirect(cols_t[:, 8 * h : 8 * h + 8]))
+            nc.vector.tensor_copy(y[:, last, block(h)], wins[last][:].indirect(cols_t[:, block(h, 8)]))
         nc.sync.dma_start(out_rows[:, last, :], y[:, last, :])
 
-        y_bf = sb("y_bf", [P, V * PACK], BF16)
+        y_bf = sb("y_bf", [P, V * PACK], BF16, tag="bias_then_rounded")
         y_c = sb("y_c", [P, V], U32)
         y_s = sb("y_s", [P, V], U8)
         y_dst = y_bf[:].rearrange("p (c t) -> p c t", t=PACK)
         y_src = y[:].rearrange("p t c -> p c t")
         nc.scalar.copy(y_dst[:, :, 0:2], y_src[:, :, 0:2])
         for h in range(2):
-            nc.vector.tensor_copy(y_dst[:, h * P : (h + 1) * P, 2:4], y_src[:, h * P : (h + 1) * P, 2:4])
+            nc.vector.tensor_copy(y_dst[:, block(h), 2:4], y_src[:, block(h), 2:4])
         for h in range(2):
-            quant(y_c, y_s, y_bf[:, h * P * PACK : (h + 1) * P * PACK], h * P, (h + 1) * P)
+            quant(y_c, y_s, y_bf[:, block(h, QUARTER)], h * P, (h + 1) * P)
         nc.sync.dma_start(out_1[0].rearrange("p c r -> p (c r)").bitcast(I32), y_c[:].bitcast(I32))
         for q in range(4):
             eng = nc.scalar if q % 2 == 0 else nc.sync

@@ -94,7 +94,8 @@ def tile_picked_selmom_none_po_kernel(
                 gs[h].rearrange("p (c i s) -> p c s i", s=PACK, i=16),
             )
         for a in range(1, 4):
-            nc.sync.dma_start(ds[a:P:32, :].bitcast(I32), ds[8 * a : P : 32, :].bitcast(I32))
+            queue = nc.scalar if a == 3 else nc.sync
+            queue.dma_start(ds[a:P:32, :].bitcast(I32), ds[8 * a : P : 32, :].bitcast(I32))
 
         wb_hi = by_row(shared.tile([P, QUARTER], F32, name="wb_hi", offset=0)[:])
         wa_raw = [
@@ -163,6 +164,7 @@ def tile_picked_selmom_none_po_kernel(
         weigh(z2_bf[:, block(0, QUARTER)], b_acc[0], gi_t)
         quant_b(3)
         project_b(3)
+        keep_warm("bank_b0")
         weigh(z2_bf[:, block(1, QUARTER)], b_acc[1], gi_t)
         keep_warm("bank_b1")
 
@@ -177,14 +179,20 @@ def tile_picked_selmom_none_po_kernel(
         z2_s = [sb("z2_s%d" % h, [P, HALF], U8) for h in range(2)]
         z2_c = [sb("z2_c0", [P, HALF], U32)]
         quant(z2_c[0], z2_s[0], z2_bf[:, block(0, 2 * QUARTER)], 0, HALF)
-        weigh(z2_bf[:, block(3, QUARTER)], b_acc[3], gi_t)
-        keep_warm("bank_b3")
-        nc.scalar.copy(wa_view[:, 64:128], wa_src[1])
+        nc.scalar.copy(wa_view[:, 64:104], wa_src[1][:, 0:40])
+        nc.vector.tensor_copy(wa_view[:, 104:128], wa_src[1][:, 40:64])
+        rows_b = shared.tile([P, PACK, P], BF16, name="rows_b", offset=3 * QUARTER * 4)
+        for s in range(PACK):
+            nc.scalar.activation(rows_b[:, s, :], b_acc[3][:, s, :], COPY, scale=gi_t[:, s : s + 1])
+        nc.scalar.copy(
+            z2_bf[:, block(3, QUARTER)].rearrange("p (c i s) -> p c s i", i=4, s=PACK),
+            rows_b[:].rearrange("p s (c i) -> p c s i", i=4),
+        )
         quant(wa_c, wa_s, wa_bf[:, block(0, QUARTER)], 0, P)
         quant(wa_c, wa_s, wa_bf[:, block(1, 2 * QUARTER)], HALF, H)
         quant(wa_c, wa_s, wa_bf[:, block(1, QUARTER)], P, HALF)
         z2_c.append(sb("z2_c1", [P, HALF], U32, tag="weights_then_codes"))
-        quant(z2_c[1], z2_s[1], z2_bf[:, block(1, 2 * QUARTER)], 0, HALF)
+        quant(z2_c[1], z2_s[1], z2_bf[:, block(2, QUARTER)], 0, P)
 
         z_lo = sb("z_lo", [P, HALF * PACK], BF16)
         z_hi = sb("z_hi", [P, HALF * PACK], BF16, tag="factor_then_result")
@@ -219,6 +227,7 @@ def tile_picked_selmom_none_po_kernel(
         weigh(z_lo[:, block(0, QUARTER)], a_acc[0], gt_t)
         weigh(z_lo[:, block(1, QUARTER)], a_acc[1], gt_t)
         quant(z_c, z_s, z_lo[:, block(0, QUARTER)], 0, P)
+        quant(z2_c[1], z2_s[1], z2_bf[:, block(3, QUARTER)], P, HALF)
         moments(0)
         interleave(nc.vector.tensor_copy, 0)
         quant(z_c, z_s, z_lo[:, block(1, QUARTER)], P, HALF)

@@ -57,12 +57,14 @@ def tile_picked_selmom_none_po_kernel(
         gi_t = sb("gi_t", [P, PACK], F32)
         xs = sb("xs", [P, T], U8, tag="bytes_then_words")
         xw = sb("xw", [P, T], U32, tag="words_then_codes")
-        nc.sync.dma_start(
-            xs[:].bitcast(I32),
-            x_scales[0].bitcast(I32).rearrange("q (o c) -> q o c", o=1).broadcast_to([16, 8, T // 4]),
-        )
+        words = x_words[0].rearrange("p c r -> p (c r)").bitcast(I32)
+        nc.gpsimd.memset(xs[:, 0 : 5 * HALF].bitcast(I32), 0)
+        nc.vector.memset(xs[:, 5 * HALF : T].bitcast(I32), 0)
         nc.sync.dma_start(offs_t[:], offs)
-        nc.sync.dma_start(xw[:].bitcast(I32), x_words[0].rearrange("p c r -> p (c r)").bitcast(I32))
+        nc.sync.dma_start(xw[:, 0:QUARTER].bitcast(I32), words[:, 0:QUARTER])
+        for r, queue in enumerate((nc.sync, nc.scalar)):
+            queue.dma_start(xs[r:P:16, :].bitcast(I32), x_scales[0][r:16:2, :].bitcast(I32))
+        nc.sync.dma_start(xw[:, QUARTER:T].bitcast(I32), words[:, QUARTER:T])
         nc.scalar.dma_start(gi_t[:], gi.rearrange("(p s) o -> p (s o)", s=PACK))
         nc.scalar.dma_start(gt_t[:], gt.rearrange("(p s) o -> p (s o)", s=PACK))
 
@@ -81,6 +83,8 @@ def tile_picked_selmom_none_po_kernel(
         wb_mid = by_row(sb("wb_mid", [P, 2 * QUARTER], F32)[:])
         nc.sync.dma_start(wb_lo, wb_rows[:, :, block(0)])
         nc.sync.dma_start(wb_mid, wb_rows[:, :, P : 3 * P])
+        wb_hi = by_row(sb("wb_hi", [P, QUARTER], F32)[:])
+        nc.sync.dma_start(wb_hi, wb_rows[:, :, block(3)])
         nc.sync.dma_start(cols_t[:], cols)
 
         gs_room = shared.tile([P, 5 * QUARTER * 4], U8, name="gs_room", offset=0)
@@ -93,16 +97,13 @@ def tile_picked_selmom_none_po_kernel(
                 ds[:].rearrange("p (s c i) -> p c s i", s=PACK, i=16)[:, block(h, 4)],
                 gs[h].rearrange("p (c i s) -> p c s i", s=PACK, i=16),
             )
-        for a in range(1, 4):
-            queue = nc.scalar if a == 3 else nc.sync
-            queue.dma_start(ds[a:P:32, :].bitcast(I32), ds[8 * a : P : 32, :].bitcast(I32))
+        for r, queue in enumerate((nc.sync, nc.scalar)):
+            queue.dma_start(ds[2 + r : P : 32, :].bitcast(I32), ds[16 + r : P : 32, :].bitcast(I32))
 
-        wb_hi = by_row(shared.tile([P, QUARTER], F32, name="wb_hi", offset=0)[:])
         wa_raw = [
             by_row(shared.tile([P, 2 * QUARTER], F32, name="wa_raw%d" % h, offset=(1 + 2 * h) * QUARTER * 4)[:])
             for h in range(2)
         ]
-        nc.sync.dma_start(wb_hi, wb_rows[:, :, block(3)])
         for h in range(2):
             nc.sync.dma_start(wa_raw[h], wa_rows[:, :, block(h, HALF)])
         wb_raw = [wb_lo, wb_mid[:, :, block(0)], wb_mid[:, :, block(1)], wb_hi]
@@ -179,8 +180,8 @@ def tile_picked_selmom_none_po_kernel(
         z2_s = [sb("z2_s%d" % h, [P, HALF], U8) for h in range(2)]
         z2_c = [sb("z2_c0", [P, HALF], U32)]
         quant(z2_c[0], z2_s[0], z2_bf[:, block(0, 2 * QUARTER)], 0, HALF)
-        nc.scalar.copy(wa_view[:, 64:104], wa_src[1][:, 0:40])
-        nc.vector.tensor_copy(wa_view[:, 104:128], wa_src[1][:, 40:64])
+        nc.scalar.copy(wa_view[:, 64:116], wa_src[1][:, 0:52])
+        nc.vector.tensor_copy(wa_view[:, 116:128], wa_src[1][:, 52:64])
         rows_b = shared.tile([P, PACK, P], BF16, name="rows_b", offset=3 * QUARTER * 4)
         for s in range(PACK):
             nc.scalar.activation(rows_b[:, s, :], b_acc[3][:, s, :], COPY, scale=gi_t[:, s : s + 1])

@@ -19,7 +19,18 @@ MULT = mybir.AluOpType.mult
 P = 128
 PACK = 4
 HALF = 256
-QUARTER = P * PACK
+SPAN = P * PACK
+BLOCK = 32
+GROUP = 16
+QUADRANT = 32
+SCALE_ROWS = 4
+F32_BYTES = 4
+RUN = 4
+BYTE_RUN = 16
+
+CLEARED_BY_GPSIMD = 5 * T // 8
+EARLY_WORDS = T // 4
+WA_BY_VECTOR = 28
 
 
 def tile_picked_selmom_none_po_kernel(
@@ -28,48 +39,55 @@ def tile_picked_selmom_none_po_kernel(
     nc = tc.nc
     with ExitStack() as ctx:
         keep = ctx.enter_context(tc.tile_pool(name="keep", bufs=1))
-        shared = ctx.enter_context(tc.tile_pool(name="shared", bufs=1))
+        reused = ctx.enter_context(tc.tile_pool(name="reused", bufs=1))
         psum = ctx.enter_context(tc.psum_pool(name="psum", bufs=1))
 
         def sb(name, shape, dtype, tag=None):
             return keep.tile(shape, dtype, name=name, tag=tag or name, align_bytes=64)
 
-        def quant(codes, scales, src, lo, hi):
-            nc.vector.quantize_mx(out=codes[:, lo:hi].bitcast(FP8X4), scales=scales[:, lo:hi], in_=src)
+        def block(i, width=P):
+            return slice(i * width, (i + 1) * width)
 
-        def product(out, lhs_c, lhs_s, lhs_cols, rhs_c, rhs_s, rhs_cols):
+        def quant(codes, scales, columns, interleaved):
+            nc.vector.quantize_mx(out=codes[:, columns].bitcast(FP8X4), scales=scales[:, columns], in_=interleaved)
+
+        def product(out, lhs_codes, lhs_scales, lhs_columns, rhs_codes, rhs_scales, rhs_columns):
             nc.tensor.matmul_mx(
                 out=out,
-                lhsT=lhs_c[:, lhs_cols].bitcast(FP8X4),
-                lhsT_scale=lhs_s[:, lhs_cols],
-                rhs=rhs_c[:, rhs_cols].bitcast(FP8X4),
-                rhs_scale=rhs_s[:, rhs_cols],
+                lhsT=lhs_codes[:, lhs_columns].bitcast(FP8X4),
+                lhsT_scale=lhs_scales[:, lhs_columns],
+                rhs=rhs_codes[:, rhs_columns].bitcast(FP8X4),
+                rhs_scale=rhs_scales[:, rhs_columns],
                 start=True,
                 stop=True,
             )
 
-        def block(i, width=P):
-            return slice(i * width, (i + 1) * width)
+        def interleave(copy, interleaved, rows):
+            copy(
+                interleaved.rearrange("p (c i j) -> p c j i", i=RUN, j=PACK),
+                rows.rearrange("p j (c i) -> p c j i", i=RUN),
+            )
 
-        offs_t = sb("offs_t", [P, S // 16], U16)
-        cols_t = sb("cols_t", [P, V // 16], U16)
+        offs_t = sb("offs_t", [P, S // GROUP], U16)
+        cols_t = sb("cols_t", [P, V // GROUP], U16)
         gt_t = sb("gt_t", [P, PACK], F32)
         gi_t = sb("gi_t", [P, PACK], F32)
-        xs = sb("xs", [P, T], U8, tag="bytes_then_words")
-        xw = sb("xw", [P, T], U32, tag="words_then_codes")
-        words = x_words[0].rearrange("p c r -> p (c r)").bitcast(I32)
-        nc.gpsimd.memset(xs[:, 0 : 5 * HALF].bitcast(I32), 0)
-        nc.vector.memset(xs[:, 5 * HALF : T].bitcast(I32), 0)
+        scale_table = sb("scale_table", [P, T], U8, tag="scales_then_picked_words")
+        word_table = sb("word_table", [P, T], U32, tag="words_then_wb_codes")
+        words_hbm = x_words[0].rearrange("p c r -> p (c r)").bitcast(I32)
+
+        nc.gpsimd.memset(scale_table[:, 0:CLEARED_BY_GPSIMD].bitcast(I32), 0)
+        nc.vector.memset(scale_table[:, CLEARED_BY_GPSIMD:T].bitcast(I32), 0)
         nc.sync.dma_start(offs_t[:], offs)
-        nc.sync.dma_start(xw[:, 0:QUARTER].bitcast(I32), words[:, 0:QUARTER])
-        for r, queue in enumerate((nc.sync, nc.scalar)):
-            queue.dma_start(xs[r:P:16, :].bitcast(I32), x_scales[0][r:16:2, :].bitcast(I32))
-        nc.sync.dma_start(xw[:, QUARTER:T].bitcast(I32), words[:, QUARTER:T])
+        nc.sync.dma_start(word_table[:, 0:EARLY_WORDS].bitcast(I32), words_hbm[:, 0:EARLY_WORDS])
+        for odd, queue in enumerate((nc.sync, nc.scalar)):
+            queue.dma_start(scale_table[odd:P:GROUP, :].bitcast(I32), x_scales[0][odd : K // BLOCK : 2, :].bitcast(I32))
+        nc.sync.dma_start(word_table[:, EARLY_WORDS:T].bitcast(I32), words_hbm[:, EARLY_WORDS:T])
         nc.scalar.dma_start(gi_t[:], gi.rearrange("(p s) o -> p (s o)", s=PACK))
         nc.scalar.dma_start(gt_t[:], gt.rearrange("(p s) o -> p (s o)", s=PACK))
 
         zero = sb("zero", [P, 1], F32)
-        bias = sb("bias", [P, 1], F32, tag="bias_then_rounded")
+        bias = sb("bias", [P, 1], F32, tag="bias_then_rounded_result")
         nc.vector.memset(zero[:], 0.0)
         nc.scalar.activation(bias[:], zero[:], TANH)
 
@@ -79,177 +97,168 @@ def tile_picked_selmom_none_po_kernel(
         def by_row(flat):
             return flat.rearrange("p (j c) -> p j c", j=PACK)
 
-        wb_lo = by_row(sb("wb_lo", [P, QUARTER], F32)[:])
-        wb_mid = by_row(sb("wb_mid", [P, 2 * QUARTER], F32)[:])
-        nc.sync.dma_start(wb_lo, wb_rows[:, :, block(0)])
-        nc.sync.dma_start(wb_mid, wb_rows[:, :, P : 3 * P])
-        wb_hi = by_row(sb("wb_hi", [P, QUARTER], F32)[:])
-        nc.sync.dma_start(wb_hi, wb_rows[:, :, block(3)])
+        wb_first = by_row(sb("wb_first", [P, SPAN], F32)[:])
+        wb_middle = by_row(sb("wb_middle", [P, 2 * SPAN], F32)[:])
+        nc.sync.dma_start(wb_first, wb_rows[:, :, block(0)])
+        nc.sync.dma_start(wb_middle, wb_rows[:, :, P : 3 * P])
+        wb_last = by_row(sb("wb_last", [P, SPAN], F32)[:])
+        nc.sync.dma_start(wb_last, wb_rows[:, :, block(3)])
         nc.sync.dma_start(cols_t[:], cols)
+        wb_raw = [wb_first, wb_middle[:, :, block(0)], wb_middle[:, :, block(1)], wb_last]
 
-        gs_room = shared.tile([P, 5 * QUARTER * 4], U8, name="gs_room", offset=0)
-        gs = [gs_room[:, block(h, HALF)] for h in range(2)]
-        ds = sb("ds", [P, S], U8)
+        picked_room = reused.tile([P, PACK * H * F32_BYTES], U8, name="picked_room", offset=0)
+        picked_scales = [picked_room[:, block(h, HALF)] for h in range(2)]
+        x_s = sb("x_s", [P, S], U8)
         for h in range(2):
-            nc.vector.tensor_copy(gs[h], xs[:].indirect(offs_t[:, block(h, 16)]))
+            nc.vector.tensor_copy(picked_scales[h], scale_table[:].indirect(offs_t[:, block(h, HALF // GROUP)]))
         for h in range(2):
             nc.vector.tensor_copy(
-                ds[:].rearrange("p (s c i) -> p c s i", s=PACK, i=16)[:, block(h, 4)],
-                gs[h].rearrange("p (c i s) -> p c s i", s=PACK, i=16),
+                x_s[:].rearrange("p (s c i) -> p c s i", s=PACK, i=BYTE_RUN)[:, block(h, HALF // PACK // BYTE_RUN)],
+                picked_scales[h].rearrange("p (c i s) -> p c s i", s=PACK, i=BYTE_RUN),
             )
-        for r, queue in enumerate((nc.sync, nc.scalar)):
-            queue.dma_start(ds[2 + r : P : 32, :].bitcast(I32), ds[16 + r : P : 32, :].bitcast(I32))
+        for odd, queue in enumerate((nc.sync, nc.scalar)):
+            queue.dma_start(
+                x_s[2 + odd : P : QUADRANT, :].bitcast(I32), x_s[GROUP + odd : P : QUADRANT, :].bitcast(I32)
+            )
 
-        wa_raw = [
-            by_row(shared.tile([P, 2 * QUARTER], F32, name="wa_raw%d" % h, offset=(1 + 2 * h) * QUARTER * 4)[:])
-            for h in range(2)
-        ]
+        wa_raw = []
         for h in range(2):
+            raw = reused.tile([P, PACK * HALF], F32, name="wa_raw%d" % h, offset=h * PACK * HALF * F32_BYTES)
+            wa_raw.append(by_row(raw[:]))
             nc.sync.dma_start(wa_raw[h], wa_rows[:, :, block(h, HALF)])
-        wb_raw = [wb_lo, wb_mid[:, :, block(0)], wb_mid[:, :, block(1)], wb_hi]
 
-        gw = sb("gw", [P, S], U32, tag="bytes_then_words")
-        dw = sb("dw", [P, S], U32)
-        nc.vector.tensor_copy(gw[:], xw[:].indirect(offs_t[:]))
+        picked_words = sb("picked_words", [P, S], U32, tag="scales_then_picked_words")
+        x_c = sb("x_c", [P, S], U32)
+        nc.vector.tensor_copy(picked_words[:], word_table[:].indirect(offs_t[:]))
 
-        wb_bf = [sb("wb_bf%d" % c, [P, QUARTER], BF16) for c in range(4)]
-        wb_c = sb("wb_c", [P, N], U32, tag="words_then_codes")
-        wb_s = sb("wb_s", [P, N], U8)
-        z2_bf = sb("z2_bf", [P, N * PACK], BF16)
-
-        def weave_b(eng, c):
-            eng(
-                wb_bf[c][:].rearrange("p (c i j) -> p c j i", i=4, j=PACK),
-                wb_raw[c].rearrange("p j (c i) -> p c j i", i=4),
-            )
-
-        def quant_b(c):
-            quant(wb_c, wb_s, wb_bf[c][:], c * P, (c + 1) * P)
-
-        def project_b(c):
-            b_acc.append(project("bank_b%d" % c, wb_c, wb_s, c))
-
-        def project(name, codes, scales, c):
-            acc = psum.tile([P, PACK, P], F32, name=name)
+        def project(bank, codes, scales, c):
+            acc = psum.tile([P, PACK, P], F32, name=bank)
             for s in range(PACK):
-                product(acc[:, s, :], dw, ds, block(s), codes, scales, block(c))
+                product(acc[:, s, :], x_c, x_s, block(s), codes, scales, block(c))
             return acc
 
-        def weigh(dst, acc, gate):
+        def weigh(interleaved, acc, gate):
             nc.vector.tensor_tensor(
-                dst.rearrange("p (m s) -> p m s", s=PACK),
+                interleaved.rearrange("p (m s) -> p m s", s=PACK),
                 acc[:].rearrange("p s m -> p m s"),
                 gate[:].rearrange("p (o s) -> p o s", o=1).broadcast_to([P, P, PACK]),
                 MULT,
             )
 
+        wb_bf = [sb("wb_bf%d" % c, [P, SPAN], BF16) for c in range(N // P)]
+        wb_c = sb("wb_c", [P, N], U32, tag="words_then_wb_codes")
+        wb_s = sb("wb_s", [P, N], U8)
+        z2_bf = sb("z2_bf", [P, N * PACK], BF16)
+        b_acc = []
+
+        def quant_wb(c):
+            quant(wb_c, wb_s, block(c), wb_bf[c][:])
+
+        def project_b(c):
+            b_acc.append(project("bank_b%d" % c, wb_c, wb_s, c))
+
         def keep_warm(bank):
             spare = psum.tile([P, N], F32, name=bank)
-            product(spare[:], dw, ds, block(0), wb_c, wb_s, slice(0, N))
+            product(spare[:], x_c, x_s, block(0), wb_c, wb_s, slice(0, N))
 
-        b_acc = []
-        weave_b(nc.scalar.copy, 0)
-        weave_b(nc.scalar.copy, 1)
-        weave_b(nc.scalar.copy, 3)
-        quant_b(0)
+        for c in (0, 1, 3):
+            interleave(nc.scalar.copy, wb_bf[c][:], wb_raw[c])
+        quant_wb(0)
         for u in range(2):
             nc.vector.tensor_copy(
-                dw[:].bitcast(I32).rearrange("p (s c i) -> p c s i", s=PACK, i=4)[:, :, block(u, 2)],
-                gw[:].bitcast(I32).rearrange("p (c i s) -> p c s i", s=PACK, i=4)[:, :, block(u, 2)],
+                x_c[:].bitcast(I32).rearrange("p (s c i) -> p c s i", s=PACK, i=RUN)[:, :, block(u, 2)],
+                picked_words[:].bitcast(I32).rearrange("p (c i s) -> p c s i", s=PACK, i=RUN)[:, :, block(u, 2)],
             )
         project_b(0)
-        weave_b(nc.vector.tensor_copy, 2)
+        interleave(nc.vector.tensor_copy, wb_bf[2][:], wb_raw[2])
         for c in (1, 2):
-            quant_b(c)
+            quant_wb(c)
             project_b(c)
-        weigh(z2_bf[:, block(0, QUARTER)], b_acc[0], gi_t)
-        quant_b(3)
+        weigh(z2_bf[:, block(0, SPAN)], b_acc[0], gi_t)
+        quant_wb(3)
         project_b(3)
         keep_warm("bank_b0")
-        weigh(z2_bf[:, block(1, QUARTER)], b_acc[1], gi_t)
+        weigh(z2_bf[:, block(1, SPAN)], b_acc[1], gi_t)
         keep_warm("bank_b1")
 
-        wa_bf = sb("wa_bf", [P, H * PACK], BF16, tag="weights_then_codes")
+        wa_bf = sb("wa_bf", [P, H * PACK], BF16, tag="rounded_wa_then_z2_codes")
         wa_c = sb("wa_c", [P, H], U32)
         wa_s = sb("wa_s", [P, H], U8)
-        wa_view = wa_bf[:].rearrange("p (t m j) -> p m j t", t=PACK, j=PACK)
+        wa_dealt = wa_bf[:].rearrange("p (t m j) -> p m j t", t=PACK, j=PACK)
         wa_src = [raw.rearrange("p j (m t) -> p m j t", t=PACK) for raw in wa_raw]
-        nc.scalar.copy(wa_view[:, 0:64], wa_src[0])
-        weigh(z2_bf[:, block(2, QUARTER)], b_acc[2], gi_t)
+        per_half = HALF // PACK
+        nc.scalar.copy(wa_dealt[:, 0:per_half], wa_src[0])
+
+        weigh(z2_bf[:, block(2, SPAN)], b_acc[2], gi_t)
         keep_warm("bank_b2")
         z2_s = [sb("z2_s%d" % h, [P, HALF], U8) for h in range(2)]
         z2_c = [sb("z2_c0", [P, HALF], U32)]
-        quant(z2_c[0], z2_s[0], z2_bf[:, block(0, 2 * QUARTER)], 0, HALF)
-        nc.scalar.copy(wa_view[:, 64:116], wa_src[1][:, 0:52])
-        nc.vector.tensor_copy(wa_view[:, 116:128], wa_src[1][:, 52:64])
-        rows_b = shared.tile([P, PACK, P], BF16, name="rows_b", offset=3 * QUARTER * 4)
+        quant(z2_c[0], z2_s[0], slice(0, HALF), z2_bf[:, block(0, 2 * SPAN)])
+        by_scalar = per_half - WA_BY_VECTOR
+        nc.scalar.copy(wa_dealt[:, per_half : per_half + by_scalar], wa_src[1][:, 0:by_scalar])
+        nc.vector.tensor_copy(wa_dealt[:, per_half + by_scalar : P], wa_src[1][:, by_scalar:per_half])
+
+        b_rows = reused.tile([P, PACK, P], BF16, name="b_rows", offset=PACK * HALF * F32_BYTES)
         for s in range(PACK):
-            nc.scalar.activation(rows_b[:, s, :], b_acc[3][:, s, :], COPY, scale=gi_t[:, s : s + 1])
-        nc.scalar.copy(
-            z2_bf[:, block(3, QUARTER)].rearrange("p (c i s) -> p c s i", i=4, s=PACK),
-            rows_b[:].rearrange("p s (c i) -> p c s i", i=4),
-        )
-        quant(wa_c, wa_s, wa_bf[:, block(0, QUARTER)], 0, P)
-        quant(wa_c, wa_s, wa_bf[:, block(1, 2 * QUARTER)], HALF, H)
-        quant(wa_c, wa_s, wa_bf[:, block(1, QUARTER)], P, HALF)
-        z2_c.append(sb("z2_c1", [P, HALF], U32, tag="weights_then_codes"))
-        quant(z2_c[1], z2_s[1], z2_bf[:, block(2, QUARTER)], 0, P)
+            nc.scalar.activation(b_rows[:, s, :], b_acc[3][:, s, :], COPY, scale=gi_t[:, s : s + 1])
+        interleave(nc.scalar.copy, z2_bf[:, block(3, SPAN)], b_rows[:])
+
+        quant(wa_c, wa_s, block(0), wa_bf[:, block(0, SPAN)])
+        quant(wa_c, wa_s, slice(HALF, H), wa_bf[:, block(1, 2 * SPAN)])
+        quant(wa_c, wa_s, block(1), wa_bf[:, block(1, SPAN)])
+        z2_c.append(sb("z2_c1", [P, HALF], U32, tag="rounded_wa_then_z2_codes"))
+        quant(z2_c[1], z2_s[1], block(0), z2_bf[:, block(2, SPAN)])
 
         z_lo = sb("z_lo", [P, HALF * PACK], BF16)
-        z_hi = sb("z_hi", [P, HALF * PACK], BF16, tag="factor_then_result")
+        z_hi = sb("z_hi", [P, HALF * PACK], BF16, tag="z_then_result")
         z_c = sb("z_c", [P, H], U32)
         z_s = sb("z_s", [P, H], U8)
-        planes = sb("planes", [P, PACK, HALF], BF16)
+        a_rows = sb("a_rows", [P, PACK, HALF], BF16)
         a_acc = []
         for u in range(2):
             a_acc.append(project("bank_a%d" % u, wa_c, wa_s, u))
-            acc = psum.tile([P, 2, HALF], F32, name="bank_u%d" % u)
-            for s in (2 * u, 2 * u + 1):
-                product(acc[:, s - 2 * u, :], dw, ds, block(s), wa_c, wa_s, slice(HALF, H))
-            for s in (2 * u, 2 * u + 1):
-                nc.scalar.activation(planes[:, s, :], acc[:, s - 2 * u, :], COPY, scale=gt_t[:, s : s + 1])
+            two_rows = psum.tile([P, 2, HALF], F32, name="bank_rows%d" % u)
+            for i in range(2):
+                product(two_rows[:, i, :], x_c, x_s, block(2 * u + i), wa_c, wa_s, slice(HALF, H))
+            for i in range(2):
+                s = 2 * u + i
+                nc.scalar.activation(a_rows[:, s, :], two_rows[:, i, :], COPY, scale=gt_t[:, s : s + 1])
 
-        wins = []
+        tanh_cv = []
 
         def moments(t):
             cv = psum.tile([P, N], F32, name="bank_b%d" % t)
             for h in range(2):
                 product(cv[:, block(h, HALF)], z_c, z_s, block(t), z2_c[h], z2_s[h], slice(0, HALF))
-            win = sb("win%d" % t, [P, N], F32)
-            nc.scalar.activation(win[:], cv[:], TANH, bias=bias[:], scale=0.0625)
-            wins.append(win)
+            whole_rows = sb("tanh_cv%d" % t, [P, N], F32)
+            nc.scalar.activation(whole_rows[:], cv[:], TANH, bias=bias[:], scale=0.0625)
+            tanh_cv.append(whole_rows)
 
-        def interleave(eng, u):
-            eng(
-                z_hi[:, block(u, QUARTER)].rearrange("p (c i s) -> p c s i", i=4, s=PACK),
-                planes[:, :, block(u)].rearrange("p s (c i) -> p c s i", i=4),
-            )
-
-        weigh(z_lo[:, block(0, QUARTER)], a_acc[0], gt_t)
-        weigh(z_lo[:, block(1, QUARTER)], a_acc[1], gt_t)
-        quant(z_c, z_s, z_lo[:, block(0, QUARTER)], 0, P)
-        quant(z2_c[1], z2_s[1], z2_bf[:, block(3, QUARTER)], P, HALF)
+        weigh(z_lo[:, block(0, SPAN)], a_acc[0], gt_t)
+        weigh(z_lo[:, block(1, SPAN)], a_acc[1], gt_t)
+        quant(z_c, z_s, block(0), z_lo[:, block(0, SPAN)])
+        quant(z2_c[1], z2_s[1], block(1), z2_bf[:, block(3, SPAN)])
         moments(0)
-        interleave(nc.vector.tensor_copy, 0)
-        quant(z_c, z_s, z_lo[:, block(1, QUARTER)], P, HALF)
+        interleave(nc.vector.tensor_copy, z_hi[:, block(0, SPAN)], a_rows[:, :, block(0)])
+        quant(z_c, z_s, block(1), z_lo[:, block(1, SPAN)])
         moments(1)
-        interleave(nc.vector.tensor_copy, 1)
-        quant(z_c, z_s, z_hi[:, block(0, QUARTER)], HALF, HALF + P)
+        interleave(nc.vector.tensor_copy, z_hi[:, block(1, SPAN)], a_rows[:, :, block(1)])
+        quant(z_c, z_s, block(2), z_hi[:, block(0, SPAN)])
         moments(2)
-        quant(z_c, z_s, z_hi[:, block(1, QUARTER)], HALF + P, H)
+        quant(z_c, z_s, block(3), z_hi[:, block(1, SPAN)])
         moments(3)
 
-        y = sb("y", [P, PACK, V], F32, tag="factor_then_result")
+        y = sb("y", [P, PACK, V], F32, tag="z_then_result")
         out_rows = out_0.rearrange("(p t) v -> p t v", t=PACK)
         last = PACK - 1
         for t in range(last):
-            nc.vector.tensor_copy(y[:, t, :], wins[t][:].indirect(cols_t[:]))
+            nc.vector.tensor_copy(y[:, t, :], tanh_cv[t][:].indirect(cols_t[:]))
             nc.sync.dma_start(out_rows[:, t, :], y[:, t, :])
         for h in range(2):
-            nc.vector.tensor_copy(y[:, last, block(h)], wins[last][:].indirect(cols_t[:, block(h, 8)]))
+            nc.vector.tensor_copy(y[:, last, block(h)], tanh_cv[last][:].indirect(cols_t[:, block(h, P // GROUP)]))
         nc.sync.dma_start(out_rows[:, last, :], y[:, last, :])
 
-        y_bf = sb("y_bf", [P, V * PACK], BF16, tag="bias_then_rounded")
+        y_bf = sb("y_bf", [P, V * PACK], BF16, tag="bias_then_rounded_result")
         y_c = sb("y_c", [P, V], U32)
         y_s = sb("y_s", [P, V], U8)
         y_dst = y_bf[:].rearrange("p (c t) -> p c t", t=PACK)
@@ -258,8 +267,11 @@ def tile_picked_selmom_none_po_kernel(
         for h in range(2):
             nc.vector.tensor_copy(y_dst[:, block(h), 2:4], y_src[:, block(h), 2:4])
         for h in range(2):
-            quant(y_c, y_s, y_bf[:, block(h, QUARTER)], h * P, (h + 1) * P)
+            quant(y_c, y_s, block(h), y_bf[:, block(h, SPAN)])
         nc.sync.dma_start(out_1[0].rearrange("p c r -> p (c r)").bitcast(I32), y_c[:].bitcast(I32))
-        for q in range(4):
-            eng = nc.scalar if q % 2 == 0 else nc.sync
-            eng.dma_start(out_2[0][4 * q : 4 * q + 4, :].bitcast(I32), y_s[32 * q : 32 * q + 4, :].bitcast(I32))
+        for q in range(P // QUADRANT):
+            queue = nc.scalar if q % 2 == 0 else nc.sync
+            queue.dma_start(
+                out_2[0][block(q, SCALE_ROWS), :].bitcast(I32),
+                y_s[QUADRANT * q : QUADRANT * q + SCALE_ROWS, :].bitcast(I32),
+            )

@@ -254,19 +254,17 @@ def tile_picked_selmom_none_po_kernel(
         for t in range(last):
             nc.vector.tensor_copy(y[:, t, :], tanh_cv[t][:].indirect(cols_t[:]))
             nc.sync.dma_start(out_rows[:, t, :], y[:, t, :])
-        for h in range(2):
-            nc.vector.tensor_copy(y[:, last, block(h)], tanh_cv[last][:].indirect(cols_t[:, block(h, P // GROUP)]))
+        halves = [tanh_cv[last][:].indirect(cols_t[:, block(h, P // GROUP)]) for h in range(2)]
+        nc.scalar.activation(y[:, last, block(0)], halves[0], COPY)
+        nc.vector.tensor_copy(y[:, last, block(1)], halves[1])
         nc.sync.dma_start(out_rows[:, last, :], y[:, last, :])
 
         y_bf = sb("y_bf", [P, V * PACK], BF16, tag="bias_then_rounded_result")
         y_c = sb("y_c", [P, V], U32)
         y_s = sb("y_s", [P, V], U8)
-        y_dst = y_bf[:].rearrange("p (c t) -> p c t", t=PACK)
-        y_src = y[:].rearrange("p t c -> p c t")
-        nc.scalar.copy(y_dst[:, :, 0:2], y_src[:, :, 0:2])
-        for h in range(2):
-            nc.vector.tensor_copy(y_dst[:, block(h), 2:4], y_src[:, block(h), 2:4])
-        for h in range(2):
+        interleave(nc.scalar.copy, y_bf[:, block(0, SPAN)], y[:, :, block(0)])
+        interleave(nc.vector.tensor_copy, y_bf[:, block(1, SPAN)], y[:, :, block(1)])
+        for h in (1, 0):
             quant(y_c, y_s, block(h), y_bf[:, block(h, SPAN)])
         nc.sync.dma_start(out_1[0].rearrange("p c r -> p (c r)").bitcast(I32), y_c[:].bitcast(I32))
         for q in range(P // QUADRANT):

@@ -28,7 +28,6 @@ F32_BYTES = 4
 RUN = 4
 BYTE_RUN = 16
 
-CLEARED_BY_GPSIMD = 5 * T // 8
 EARLY_WORDS = T // 4
 WA_BY_VECTOR = 28
 
@@ -76,8 +75,7 @@ def tile_picked_selmom_none_po_kernel(
         word_table = sb("word_table", [P, T], U32, tag="words_then_wb_codes")
         words_hbm = x_words[0].rearrange("p c r -> p (c r)").bitcast(I32)
 
-        nc.gpsimd.memset(scale_table[:, 0:CLEARED_BY_GPSIMD].bitcast(I32), 0)
-        nc.vector.memset(scale_table[:, CLEARED_BY_GPSIMD:T].bitcast(I32), 0)
+        nc.vector.memset(scale_table[:].bitcast(I32), 0)
         nc.sync.dma_start(offs_t[:], offs)
         nc.sync.dma_start(word_table[:, 0:EARLY_WORDS].bitcast(I32), words_hbm[:, 0:EARLY_WORDS])
         for odd, queue in enumerate((nc.sync, nc.scalar)):

@@ -15,6 +15,9 @@ FP8X4 = mybir.dt.float8_e4m3fn_x4
 TANH = mybir.ActivationFunctionType.Tanh
 COPY = mybir.ActivationFunctionType.Copy
 MULT = mybir.AluOpType.mult
+ADD = mybir.AluOpType.add
+EQUAL = mybir.AluOpType.is_equal
+AXIS_X = mybir.AxisListType.X
 
 P = 128
 PACK = 4
@@ -69,20 +72,36 @@ def tile_picked_selmom_none_po_kernel(
 
         offs_t = sb("offs_t", [P, S // GROUP], U16)
         cols_t = sb("cols_t", [P, V // GROUP], U16)
-        gt_t = sb("gt_t", [P, PACK], F32)
-        gi_t = sb("gi_t", [P, PACK], F32)
-        scale_table = sb("scale_table", [P, T], U8, tag="scales_then_picked_words")
+        gate_rows = sb("gate_rows", [P, 2, GROUP], F32)
+        table_offset = PACK * H * F32_BYTES
+        scale_table = reused.tile([P, T], U8, name="scale_table", offset=table_offset, align_bytes=64)
         word_table = sb("word_table", [P, T], U32, tag="words_then_wb_codes")
         words_hbm = x_words[0].rearrange("p c r -> p (c r)").bitcast(I32)
 
         nc.vector.memset(scale_table[:].bitcast(I32), 0)
         nc.sync.dma_start(offs_t[:], offs)
+        for i, gate in enumerate((gi, gt)):
+            sixteen = gate.rearrange("(q u e) o -> q u (e o)", u=1, e=GROUP)
+            nc.scalar.dma_start(gate_rows[:, i, :], sixteen.broadcast_to([P // RUN, RUN, GROUP]))
         nc.sync.dma_start(word_table[:, 0:EARLY_WORDS].bitcast(I32), words_hbm[:, 0:EARLY_WORDS])
         for odd, queue in enumerate((nc.sync, nc.scalar)):
             queue.dma_start(scale_table[odd:P:GROUP, :].bitcast(I32), x_scales[0][odd : K // BLOCK : 2, :].bitcast(I32))
         nc.sync.dma_start(word_table[:, EARLY_WORDS:T].bitcast(I32), words_hbm[:, EARLY_WORDS:T])
-        nc.scalar.dma_start(gi_t[:], gi.rearrange("(p s) o -> p (s o)", s=PACK))
-        nc.scalar.dma_start(gt_t[:], gt.rearrange("(p s) o -> p (s o)", s=PACK))
+
+        column_rest = sb("column_rest", [P, QUADRANT], F32)
+        partition_rest = sb("partition_rest", [P, QUADRANT], F32)
+        own = sb("own", [P, RUN], F32)
+        masked = sb("masked", [P, 2 * PACK, RUN], F32)
+        for r in range(RUN):
+            nc.vector.memset(column_rest[:, r:QUADRANT:RUN], float(r))
+        nc.vector.transpose(partition_rest[:], column_rest[:])
+        nc.vector.tensor_tensor(own[:], partition_rest[:, 0:RUN], column_rest[:, 0:RUN], EQUAL)
+        nc.vector.tensor_tensor(
+            masked[:],
+            gate_rows[:].rearrange("p g (s r) -> p (g s) r", r=RUN),
+            own[:].rearrange("p (o r) -> p o r", o=1).broadcast_to([P, 2 * PACK, RUN]),
+            MULT,
+        )
 
         zero = sb("zero", [P, 1], F32)
         bias = sb("bias", [P, 1], F32, tag="bias_then_rounded_result")
@@ -101,19 +120,19 @@ def tile_picked_selmom_none_po_kernel(
         nc.sync.dma_start(wb_middle, wb_rows[:, :, P : 3 * P])
         wb_last = by_row(sb("wb_last", [P, SPAN], F32)[:])
         nc.sync.dma_start(wb_last, wb_rows[:, :, block(3)])
-        nc.sync.dma_start(cols_t[:], cols)
         wb_raw = [wb_first, wb_middle[:, :, block(0)], wb_middle[:, :, block(1)], wb_last]
 
         picked_room = reused.tile([P, PACK * H * F32_BYTES], U8, name="picked_room", offset=0)
-        picked_scales = [picked_room[:, block(h, HALF)] for h in range(2)]
+        picked_scales = picked_room[:, 0:S]
         x_s = sb("x_s", [P, S], U8)
-        for h in range(2):
-            nc.vector.tensor_copy(picked_scales[h], scale_table[:].indirect(offs_t[:, block(h, HALF // GROUP)]))
-        for h in range(2):
-            nc.vector.tensor_copy(
-                x_s[:].rearrange("p (s c i) -> p c s i", s=PACK, i=BYTE_RUN)[:, block(h, HALF // PACK // BYTE_RUN)],
-                picked_scales[h].rearrange("p (c i s) -> p c s i", s=PACK, i=BYTE_RUN),
-            )
+        nc.vector.tensor_copy(picked_scales, scale_table[:].indirect(offs_t[:]))
+        gates = reused.tile([P, 2 * PACK], F32, name="gates", offset=table_offset)
+        gi_t, gt_t = gates[:, 0:PACK], gates[:, PACK : 2 * PACK]
+        nc.vector.tensor_reduce(gates[:], masked[:], AXIS_X, ADD)
+        nc.vector.tensor_copy(
+            x_s[:].bitcast(I32).rearrange("p (s q) -> p s q", s=PACK),
+            picked_scales.bitcast(I32).rearrange("p (q s) -> p s q", s=PACK),
+        )
         for odd, queue in enumerate((nc.sync, nc.scalar)):
             queue.dma_start(
                 x_s[2 + odd : P : QUADRANT, :].bitcast(I32), x_s[GROUP + odd : P : QUADRANT, :].bitcast(I32)
@@ -125,7 +144,9 @@ def tile_picked_selmom_none_po_kernel(
             wa_raw.append(by_row(raw[:]))
             nc.sync.dma_start(wa_raw[h], wa_rows[:, :, block(h, HALF)])
 
-        picked_words = sb("picked_words", [P, S], U32, tag="scales_then_picked_words")
+        nc.sync.dma_start(cols_t[:], cols)
+
+        picked_words = reused.tile([P, S], U32, name="picked_words", offset=table_offset + 64, align_bytes=64)
         x_c = sb("x_c", [P, S], U32)
         nc.vector.tensor_copy(picked_words[:], word_table[:].indirect(offs_t[:]))
 
@@ -139,7 +160,7 @@ def tile_picked_selmom_none_po_kernel(
             nc.vector.tensor_tensor(
                 interleaved.rearrange("p (m s) -> p m s", s=PACK),
                 acc[:].rearrange("p s m -> p m s"),
-                gate[:].rearrange("p (o s) -> p o s", o=1).broadcast_to([P, P, PACK]),
+                gate.rearrange("p (o s) -> p o s", o=1).broadcast_to([P, P, PACK]),
                 MULT,
             )
 
@@ -164,8 +185,8 @@ def tile_picked_selmom_none_po_kernel(
         quant_wb(0)
         for u in range(2):
             nc.vector.tensor_copy(
-                x_c[:].bitcast(I32).rearrange("p (s c i) -> p c s i", s=PACK, i=RUN)[:, :, block(u, 2)],
-                picked_words[:].bitcast(I32).rearrange("p (c i s) -> p c s i", s=PACK, i=RUN)[:, :, block(u, 2)],
+                x_c[:].bitcast(I32).rearrange("p (s q r) -> p q s r", s=PACK, r=RUN)[:, :, block(u, 2)],
+                picked_words[:].bitcast(I32).rearrange("p (q s r) -> p q s r", s=PACK, r=RUN)[:, :, block(u, 2)],
             )
         project_b(0)
         interleave(nc.vector.tensor_copy, wb_bf[2][:], wb_raw[2])

@@ -32,7 +32,7 @@ RUN = 4
 BYTE_RUN = 16
 
 EARLY_WORDS = T // 4
-WA_BY_VECTOR = 28
+WA_BY_VECTOR = 12
 
 
 def tile_picked_selmom_none_po_kernel(
@@ -139,10 +139,10 @@ def tile_picked_selmom_none_po_kernel(
             )
 
         wa_raw = []
-        for h in range(2):
-            raw = reused.tile([P, PACK * HALF], F32, name="wa_raw%d" % h, offset=h * PACK * HALF * F32_BYTES)
+        for c in range(H // P):
+            raw = reused.tile([P, SPAN], F32, name="wa_raw%d" % c, offset=c * SPAN * F32_BYTES)
             wa_raw.append(by_row(raw[:]))
-            nc.sync.dma_start(wa_raw[h], wa_rows[:, :, block(h, HALF)])
+            nc.sync.dma_start(wa_raw[c], wa_rows[:, :, block(c)])
 
         nc.sync.dma_start(cols_t[:], cols)
 
@@ -205,19 +205,20 @@ def tile_picked_selmom_none_po_kernel(
         wa_s = sb("wa_s", [P, H], U8)
         wa_dealt = wa_bf[:].rearrange("p (t m j) -> p m j t", t=PACK, j=PACK)
         wa_src = [raw.rearrange("p j (m t) -> p m j t", t=PACK) for raw in wa_raw]
-        per_half = HALF // PACK
-        nc.scalar.copy(wa_dealt[:, 0:per_half], wa_src[0])
+        per_load = P // PACK
+        for c in range(3):
+            nc.scalar.copy(wa_dealt[:, block(c, per_load)], wa_src[c])
 
         weigh(z2_bf[:, block(2, SPAN)], b_acc[2], gi_t)
         keep_warm("bank_b2")
         z2_s = [sb("z2_s%d" % h, [P, HALF], U8) for h in range(2)]
         z2_c = [sb("z2_c0", [P, HALF], U32)]
         quant(z2_c[0], z2_s[0], slice(0, HALF), z2_bf[:, block(0, 2 * SPAN)])
-        by_scalar = per_half - WA_BY_VECTOR
-        nc.scalar.copy(wa_dealt[:, per_half : per_half + by_scalar], wa_src[1][:, 0:by_scalar])
-        nc.vector.tensor_copy(wa_dealt[:, per_half + by_scalar : P], wa_src[1][:, by_scalar:per_half])
+        by_scalar = per_load - WA_BY_VECTOR
+        nc.scalar.copy(wa_dealt[:, 3 * per_load : P - WA_BY_VECTOR], wa_src[3][:, 0:by_scalar])
+        nc.vector.tensor_copy(wa_dealt[:, P - WA_BY_VECTOR : P], wa_src[3][:, by_scalar:per_load])
 
-        b_rows = reused.tile([P, PACK, P], BF16, name="b_rows", offset=PACK * HALF * F32_BYTES)
+        b_rows = reused.tile([P, PACK, P], BF16, name="b_rows", offset=2 * SPAN * F32_BYTES)
         for s in range(PACK):
             nc.scalar.activation(b_rows[:, s, :], b_acc[3][:, s, :], COPY, scale=gi_t[:, s : s + 1])
         interleave(nc.scalar.copy, z2_bf[:, block(3, SPAN)], b_rows[:])
@@ -272,7 +273,7 @@ def tile_picked_selmom_none_po_kernel(
         last = PACK - 1
         for t in range(last):
             nc.vector.tensor_copy(y[:, t, :], tanh_cv[t][:].indirect(cols_t[:]))
-            nc.sync.dma_start(out_rows[:, t, :], y[:, t, :])
+        nc.sync.dma_start(out_rows[:, 0:last, :], y[:, 0:last, :])
         halves = [tanh_cv[last][:].indirect(cols_t[:, block(h, P // GROUP)]) for h in range(2)]
         nc.scalar.activation(y[:, last, block(0)], halves[0], COPY)
         nc.vector.tensor_copy(y[:, last, block(1)], halves[1])

@@ -176,10 +176,6 @@ def tile_picked_selmom_none_po_kernel(
         def project_b(c):
             b_acc.append(project("bank_b%d" % c, wb_c, wb_s, c))
 
-        def keep_warm(bank):
-            spare = psum.tile([P, N], F32, name=bank)
-            product(spare[:], x_c, x_s, block(0), wb_c, wb_s, slice(0, N))
-
         for c in (0, 1, 3):
             interleave(nc.scalar.copy, wb_bf[c][:], wb_raw[c])
         quant_wb(0)
@@ -196,9 +192,7 @@ def tile_picked_selmom_none_po_kernel(
         weigh(z2_bf[:, block(0, SPAN)], b_acc[0], gi_t)
         quant_wb(3)
         project_b(3)
-        keep_warm("bank_b0")
         weigh(z2_bf[:, block(1, SPAN)], b_acc[1], gi_t)
-        keep_warm("bank_b1")
 
         wa_bf = sb("wa_bf", [P, H * PACK], BF16, tag="rounded_wa_then_z2_codes")
         wa_c = sb("wa_c", [P, H], U32)
@@ -210,7 +204,6 @@ def tile_picked_selmom_none_po_kernel(
             nc.scalar.copy(wa_dealt[:, block(c, per_load)], wa_src[c])
 
         weigh(z2_bf[:, block(2, SPAN)], b_acc[2], gi_t)
-        keep_warm("bank_b2")
         z2_s = [sb("z2_s%d" % h, [P, HALF], U8) for h in range(2)]
         z2_c = [sb("z2_c0", [P, HALF], U32)]
         quant(z2_c[0], z2_s[0], slice(0, HALF), z2_bf[:, block(0, 2 * SPAN)])

@@ -194,48 +194,67 @@ def tile_picked_selmom_none_po_kernel(
         project_b(3)
         weigh(z2_bf[:, block(1, SPAN)], b_acc[1], gi_t)
 
-        wa_bf = sb("wa_bf", [P, H * PACK], BF16, tag="rounded_wa_then_z2_codes")
+        wa_bf = sb("wa_bf", [P, H * PACK], BF16)
         wa_c = sb("wa_c", [P, H], U32)
         wa_s = sb("wa_s", [P, H], U8)
-        wa_dealt = wa_bf[:].rearrange("p (t m j) -> p m j t", t=PACK, j=PACK)
-        wa_src = [raw.rearrange("p j (m t) -> p m j t", t=PACK) for raw in wa_raw]
+        wa_dealt = wa_bf[:].rearrange("p (a h b m j) -> p h m j a b", a=2, h=2, b=2, j=PACK)
+        wa_src = [raw.rearrange("p j (m a b) -> p m j a b", a=2, b=2) for raw in wa_raw]
         per_load = P // PACK
-        for c in range(3):
-            nc.scalar.copy(wa_dealt[:, block(c, per_load)], wa_src[c])
+
+        def round_wa(copy, c, first, last):
+            start = c % 2 * per_load
+            copy(wa_dealt[:, c // 2, start + first : start + last], wa_src[c][:, first:last])
+
+        for c in range(2):
+            round_wa(nc.scalar.copy, c, 0, per_load)
 
         weigh(z2_bf[:, block(2, SPAN)], b_acc[2], gi_t)
         z2_s = [sb("z2_s%d" % h, [P, HALF], U8) for h in range(2)]
         z2_c = [sb("z2_c0", [P, HALF], U32)]
-        quant(z2_c[0], z2_s[0], slice(0, HALF), z2_bf[:, block(0, 2 * SPAN)])
+        quant(wa_c, wa_s, block(0), wa_bf[:, block(0, SPAN)])
+        a_acc = [project("bank_a0", wa_c, wa_s, 0)]
         by_scalar = per_load - WA_BY_VECTOR
-        nc.scalar.copy(wa_dealt[:, 3 * per_load : P - WA_BY_VECTOR], wa_src[3][:, 0:by_scalar])
-        nc.vector.tensor_copy(wa_dealt[:, P - WA_BY_VECTOR : P], wa_src[3][:, by_scalar:per_load])
+        round_wa(nc.scalar.copy, 2, 0, per_load)
+        round_wa(nc.scalar.copy, 3, 0, by_scalar)
+        round_wa(nc.vector.tensor_copy, 3, by_scalar, per_load)
+        quant(z2_c[0], z2_s[0], slice(0, HALF), z2_bf[:, block(0, 2 * SPAN)])
 
         b_rows = reused.tile([P, PACK, P], BF16, name="b_rows", offset=2 * SPAN * F32_BYTES)
         for s in range(PACK):
             nc.scalar.activation(b_rows[:, s, :], b_acc[3][:, s, :], COPY, scale=gi_t[:, s : s + 1])
         interleave(nc.scalar.copy, z2_bf[:, block(3, SPAN)], b_rows[:])
 
-        quant(wa_c, wa_s, block(0), wa_bf[:, block(0, SPAN)])
-        quant(wa_c, wa_s, slice(HALF, H), wa_bf[:, block(1, 2 * SPAN)])
         quant(wa_c, wa_s, block(1), wa_bf[:, block(1, SPAN)])
-        z2_c.append(sb("z2_c1", [P, HALF], U32, tag="rounded_wa_then_z2_codes"))
-        quant(z2_c[1], z2_s[1], block(0), z2_bf[:, block(2, SPAN)])
+        a_acc.append(project("bank_a1", wa_c, wa_s, 1))
+        quant(wa_c, wa_s, slice(HALF, H), wa_bf[:, block(1, 2 * SPAN)])
+        z2_c.append(sb("z2_c1", [P, HALF], U32))
 
-        z_lo = sb("z_lo", [P, HALF * PACK], BF16)
+        z_lo = reused.tile([P, HALF * PACK], BF16, name="z_lo", offset=3 * SPAN * F32_BYTES, align_bytes=64)
         z_hi = sb("z_hi", [P, HALF * PACK], BF16, tag="z_then_result")
         z_c = sb("z_c", [P, H], U32)
         z_s = sb("z_s", [P, H], U8)
         a_rows = sb("a_rows", [P, PACK, HALF], BF16)
-        a_acc = []
         for u in range(2):
-            a_acc.append(project("bank_a%d" % u, wa_c, wa_s, u))
             two_rows = psum.tile([P, 2, HALF], F32, name="bank_rows%d" % u)
             for i in range(2):
                 product(two_rows[:, i, :], x_c, x_s, block(2 * u + i), wa_c, wa_s, slice(HALF, H))
             for i in range(2):
                 s = 2 * u + i
                 nc.scalar.activation(a_rows[:, s, :], two_rows[:, i, :], COPY, scale=gt_t[:, s : s + 1])
+
+        def weigh_half(h):
+            nc.vector.tensor_tensor(
+                z_lo[:].rearrange("p (b h m s) -> p h b m s", b=2, h=2, s=PACK)[:, h],
+                a_acc[h][:].rearrange("p s (b m) -> p b m s", b=2),
+                gt_t.rearrange("p (b m s) -> p b m s", b=1, m=1).broadcast_to([P, 2, P // 2, PACK]),
+                MULT,
+            )
+
+        def interleave_class(b):
+            nc.vector.tensor_copy(
+                z_hi[:, block(b, SPAN)].rearrange("p (h c i j) -> p h c j i", h=2, i=RUN, j=PACK),
+                a_rows[:].rearrange("p j (h b c i) -> p b h c j i", h=2, b=2, i=RUN)[:, b],
+            )
 
         tanh_cv = []
 
@@ -247,19 +266,17 @@ def tile_picked_selmom_none_po_kernel(
             nc.scalar.activation(whole_rows[:], cv[:], TANH, bias=bias[:], scale=0.0625)
             tanh_cv.append(whole_rows)
 
-        weigh(z_lo[:, block(0, SPAN)], a_acc[0], gt_t)
-        weigh(z_lo[:, block(1, SPAN)], a_acc[1], gt_t)
-        quant(z_c, z_s, block(0), z_lo[:, block(0, SPAN)])
-        quant(z2_c[1], z2_s[1], block(1), z2_bf[:, block(3, SPAN)])
-        moments(0)
-        interleave(nc.vector.tensor_copy, z_hi[:, block(0, SPAN)], a_rows[:, :, block(0)])
-        quant(z_c, z_s, block(1), z_lo[:, block(1, SPAN)])
-        moments(1)
-        interleave(nc.vector.tensor_copy, z_hi[:, block(1, SPAN)], a_rows[:, :, block(1)])
-        quant(z_c, z_s, block(2), z_hi[:, block(0, SPAN)])
-        moments(2)
-        quant(z_c, z_s, block(3), z_hi[:, block(1, SPAN)])
-        moments(3)
+        weigh_half(0)
+        weigh_half(1)
+        quant(z2_c[1], z2_s[1], slice(0, HALF), z2_bf[:, block(1, 2 * SPAN)])
+        for t in range(2):
+            quant(z_c, z_s, block(t), z_lo[:, block(t, SPAN)])
+            moments(t)
+        for b in range(2):
+            interleave_class(b)
+        for b in range(2):
+            quant(z_c, z_s, block(2 + b), z_hi[:, block(b, SPAN)])
+            moments(2 + b)
 
         y = sb("y", [P, PACK, V], F32, tag="z_then_result")
         out_rows = out_0.rearrange("(p t) v -> p t v", t=PACK)

@@ -197,13 +197,16 @@ def tile_picked_selmom_none_po_kernel(
         wa_bf = sb("wa_bf", [P, H * PACK], BF16)
         wa_c = sb("wa_c", [P, H], U32)
         wa_s = sb("wa_s", [P, H], U8)
-        wa_dealt = wa_bf[:].rearrange("p (a h b m j) -> p h m j a b", a=2, h=2, b=2, j=PACK)
-        wa_src = [raw.rearrange("p j (m a b) -> p m j a b", a=2, b=2) for raw in wa_raw]
+        wa_dealt = wa_bf[:].rearrange("p (t m j) -> p m j t", t=PACK, j=PACK)
+        wa_src = [raw.rearrange("p j (m t) -> p m j t", t=PACK) for raw in wa_raw]
         per_load = P // PACK
 
         def round_wa(copy, c, first, last):
-            start = c % 2 * per_load
-            copy(wa_dealt[:, c // 2, start + first : start + last], wa_src[c][:, first:last])
+            copy(wa_dealt[:, c * per_load + first : c * per_load + last], wa_src[c][:, first:last])
+
+        def quant_half(h):
+            for t in range(2):
+                quant(wa_c, wa_s, block(2 * h + t, P // 2), wa_bf[:, block(2 * t + h, HALF)])
 
         for c in range(2):
             round_wa(nc.scalar.copy, c, 0, per_load)
@@ -211,7 +214,7 @@ def tile_picked_selmom_none_po_kernel(
         weigh(z2_bf[:, block(2, SPAN)], b_acc[2], gi_t)
         z2_s = [sb("z2_s%d" % h, [P, HALF], U8) for h in range(2)]
         z2_c = [sb("z2_c0", [P, HALF], U32)]
-        quant(wa_c, wa_s, block(0), wa_bf[:, block(0, SPAN)])
+        quant_half(0)
         a_acc = [project("bank_a0", wa_c, wa_s, 0)]
         by_scalar = per_load - WA_BY_VECTOR
         round_wa(nc.scalar.copy, 2, 0, per_load)
@@ -224,7 +227,7 @@ def tile_picked_selmom_none_po_kernel(
             nc.scalar.activation(b_rows[:, s, :], b_acc[3][:, s, :], COPY, scale=gi_t[:, s : s + 1])
         interleave(nc.scalar.copy, z2_bf[:, block(3, SPAN)], b_rows[:])
 
-        quant(wa_c, wa_s, block(1), wa_bf[:, block(1, SPAN)])
+        quant_half(1)
         a_acc.append(project("bank_a1", wa_c, wa_s, 1))
         quant(wa_c, wa_s, slice(HALF, H), wa_bf[:, block(1, 2 * SPAN)])
         z2_c.append(sb("z2_c1", [P, HALF], U32))
@@ -250,12 +253,6 @@ def tile_picked_selmom_none_po_kernel(
                 MULT,
             )
 
-        def interleave_class(b):
-            nc.vector.tensor_copy(
-                z_hi[:, block(b, SPAN)].rearrange("p (h c i j) -> p h c j i", h=2, i=RUN, j=PACK),
-                a_rows[:].rearrange("p j (h b c i) -> p b h c j i", h=2, b=2, i=RUN)[:, b],
-            )
-
         tanh_cv = []
 
         def moments(t):
@@ -273,7 +270,7 @@ def tile_picked_selmom_none_po_kernel(
             quant(z_c, z_s, block(t), z_lo[:, block(t, SPAN)])
             moments(t)
         for b in range(2):
-            interleave_class(b)
+            interleave(nc.vector.tensor_copy, z_hi[:, block(b, SPAN)], a_rows[:, :, block(b)])
         for b in range(2):
             quant(z_c, z_s, block(2 + b), z_hi[:, block(b, SPAN)])
             moments(2 + b)

@@ -236,14 +236,12 @@ def tile_picked_selmom_none_po_kernel(
         z_hi = sb("z_hi", [P, HALF * PACK], BF16, tag="z_then_result")
         z_c = sb("z_c", [P, H], U32)
         z_s = sb("z_s", [P, H], U8)
-        a_rows = sb("a_rows", [P, PACK, HALF], BF16)
-        for u in range(2):
-            two_rows = psum.tile([P, 2, HALF], F32, name="bank_rows%d" % u)
-            for i in range(2):
-                product(two_rows[:, i, :], x_c, x_s, block(2 * u + i), wa_c, wa_s, slice(HALF, H))
-            for i in range(2):
-                s = 2 * u + i
-                nc.scalar.activation(a_rows[:, s, :], two_rows[:, i, :], COPY, scale=gt_t[:, s : s + 1])
+        a_rows = []
+        for t in (2, 3):
+            acc = project("bank_a%d" % t, wa_c, wa_s, t)
+            a_rows.append(sb("a_rows%d" % t, [P, PACK, P], BF16))
+            for s in range(PACK):
+                nc.scalar.activation(a_rows[-1][:, s, :], acc[:, s, :], COPY, scale=gt_t[:, s : s + 1])
 
         def weigh_half(h):
             nc.vector.tensor_tensor(
@@ -266,14 +264,16 @@ def tile_picked_selmom_none_po_kernel(
         weigh_half(0)
         weigh_half(1)
         quant(z2_c[1], z2_s[1], slice(0, HALF), z2_bf[:, block(1, 2 * SPAN)])
-        for t in range(2):
-            quant(z_c, z_s, block(t), z_lo[:, block(t, SPAN)])
-            moments(t)
-        for b in range(2):
-            interleave(nc.vector.tensor_copy, z_hi[:, block(b, SPAN)], a_rows[:, :, block(b)])
-        for b in range(2):
-            quant(z_c, z_s, block(2 + b), z_hi[:, block(b, SPAN)])
-            moments(2 + b)
+        quant(z_c, z_s, block(0), z_lo[:, block(0, SPAN)])
+        moments(0)
+        interleave(nc.vector.tensor_copy, z_hi[:, block(0, SPAN)], a_rows[0][:])
+        quant(z_c, z_s, block(1), z_lo[:, block(1, SPAN)])
+        moments(1)
+        quant(z_c, z_s, block(2), z_hi[:, block(0, SPAN)])
+        moments(2)
+        interleave(nc.vector.tensor_copy, z_hi[:, block(1, SPAN)], a_rows[1][:])
+        quant(z_c, z_s, block(3), z_hi[:, block(1, SPAN)])
+        moments(3)
 
         y = sb("y", [P, PACK, V], F32, tag="z_then_result")
         out_rows = out_0.rearrange("(p t) v -> p t v", t=PACK)

@@ -194,7 +194,7 @@ def tile_picked_selmom_none_po_kernel(
         project_b(3)
         weigh(z2_bf[:, block(1, SPAN)], b_acc[1], gi_t)
 
-        wa_bf = sb("wa_bf", [P, H * PACK], BF16)
+        wa_bf = sb("wa_bf", [P, H * PACK], BF16, tag="rounded_wa_then_z2_codes")
         wa_c = sb("wa_c", [P, H], U32)
         wa_s = sb("wa_s", [P, H], U8)
         wa_dealt = wa_bf[:].rearrange("p (t m j) -> p m j t", t=PACK, j=PACK)
@@ -216,32 +216,27 @@ def tile_picked_selmom_none_po_kernel(
         z2_c = [sb("z2_c0", [P, HALF], U32)]
         quant_half(0)
         a_acc = [project("bank_a0", wa_c, wa_s, 0)]
+        weigh(z2_bf[:, block(3, SPAN)], b_acc[3], gi_t)
         by_scalar = per_load - WA_BY_VECTOR
         round_wa(nc.scalar.copy, 2, 0, per_load)
         round_wa(nc.scalar.copy, 3, 0, by_scalar)
         round_wa(nc.vector.tensor_copy, 3, by_scalar, per_load)
         quant(z2_c[0], z2_s[0], slice(0, HALF), z2_bf[:, block(0, 2 * SPAN)])
 
-        b_rows = reused.tile([P, PACK, P], BF16, name="b_rows", offset=2 * SPAN * F32_BYTES)
-        for s in range(PACK):
-            nc.scalar.activation(b_rows[:, s, :], b_acc[3][:, s, :], COPY, scale=gi_t[:, s : s + 1])
-        interleave(nc.scalar.copy, z2_bf[:, block(3, SPAN)], b_rows[:])
-
         quant_half(1)
         a_acc.append(project("bank_a1", wa_c, wa_s, 1))
         quant(wa_c, wa_s, slice(HALF, H), wa_bf[:, block(1, 2 * SPAN)])
-        z2_c.append(sb("z2_c1", [P, HALF], U32))
+        z2_c.append(sb("z2_c1", [P, HALF], U32, tag="rounded_wa_then_z2_codes"))
 
         z_lo = reused.tile([P, HALF * PACK], BF16, name="z_lo", offset=3 * SPAN * F32_BYTES, align_bytes=64)
         z_hi = sb("z_hi", [P, HALF * PACK], BF16, tag="z_then_result")
         z_c = sb("z_c", [P, H], U32)
         z_s = sb("z_s", [P, H], U8)
-        a_rows = []
-        for t in (2, 3):
-            acc = project("bank_a%d" % t, wa_c, wa_s, t)
-            a_rows.append(sb("a_rows%d" % t, [P, PACK, P], BF16))
-            for s in range(PACK):
-                nc.scalar.activation(a_rows[-1][:, s, :], acc[:, s, :], COPY, scale=gt_t[:, s : s + 1])
+        last_class = project("bank_a3", wa_c, wa_s, 3)
+        a_rows = sb("a_rows", [P, PACK, P], BF16)
+        for s in range(PACK):
+            nc.scalar.activation(a_rows[:, s, :], last_class[:, s, :], COPY, scale=gt_t[:, s : s + 1])
+        third_class = project("bank_a2", wa_c, wa_s, 2)
 
         def weigh_half(h):
             nc.vector.tensor_tensor(
@@ -264,16 +259,14 @@ def tile_picked_selmom_none_po_kernel(
         weigh_half(0)
         weigh_half(1)
         quant(z2_c[1], z2_s[1], slice(0, HALF), z2_bf[:, block(1, 2 * SPAN)])
-        quant(z_c, z_s, block(0), z_lo[:, block(0, SPAN)])
-        moments(0)
-        interleave(nc.vector.tensor_copy, z_hi[:, block(0, SPAN)], a_rows[0][:])
-        quant(z_c, z_s, block(1), z_lo[:, block(1, SPAN)])
-        moments(1)
-        quant(z_c, z_s, block(2), z_hi[:, block(0, SPAN)])
-        moments(2)
-        interleave(nc.vector.tensor_copy, z_hi[:, block(1, SPAN)], a_rows[1][:])
-        quant(z_c, z_s, block(3), z_hi[:, block(1, SPAN)])
-        moments(3)
+        for t in range(2):
+            quant(z_c, z_s, block(t), z_lo[:, block(t, SPAN)])
+            moments(t)
+        weigh(z_hi[:, block(0, SPAN)], third_class, gt_t)
+        interleave(nc.vector.tensor_copy, z_hi[:, block(1, SPAN)], a_rows[:])
+        for t in range(2):
+            quant(z_c, z_s, block(2 + t), z_hi[:, block(t, SPAN)])
+            moments(2 + t)
 
         y = sb("y", [P, PACK, V], F32, tag="z_then_result")
         out_rows = out_0.rearrange("(p t) v -> p t v", t=PACK)

@@ -216,12 +216,16 @@ def tile_picked_selmom_none_po_kernel(
         z2_c = [sb("z2_c0", [P, HALF], U32)]
         quant_half(0)
         a_acc = [project("bank_a0", wa_c, wa_s, 0)]
-        weigh(z2_bf[:, block(3, SPAN)], b_acc[3], gi_t)
         by_scalar = per_load - WA_BY_VECTOR
         round_wa(nc.scalar.copy, 2, 0, per_load)
         round_wa(nc.scalar.copy, 3, 0, by_scalar)
         round_wa(nc.vector.tensor_copy, 3, by_scalar, per_load)
         quant(z2_c[0], z2_s[0], slice(0, HALF), z2_bf[:, block(0, 2 * SPAN)])
+
+        b_rows = reused.tile([P, PACK, P], BF16, name="b_rows", offset=2 * SPAN * F32_BYTES)
+        for s in range(PACK):
+            nc.scalar.activation(b_rows[:, s, :], b_acc[3][:, s, :], COPY, scale=gi_t[:, s : s + 1])
+        interleave(nc.scalar.copy, z2_bf[:, block(3, SPAN)], b_rows[:])
 
         quant_half(1)
         a_acc.append(project("bank_a1", wa_c, wa_s, 1))

@@ -31,7 +31,7 @@ F32_BYTES = 4
 RUN = 4
 BYTE_RUN = 16
 
-EARLY_WORDS = T // 4
+EARLY_WORDS = T // 8
 WA_BY_VECTOR = 12
 
 

@@ -32,7 +32,7 @@ RUN = 4
 BYTE_RUN = 16
 
 EARLY_WORDS = T // 8
-WA_BY_VECTOR = 12
+LINE = 64
 
 
 def tile_picked_selmom_none_po_kernel(
@@ -73,7 +73,7 @@ def tile_picked_selmom_none_po_kernel(
         offs_t = sb("offs_t", [P, S // GROUP], U16)
         cols_t = sb("cols_t", [P, V // GROUP], U16)
         gate_rows = sb("gate_rows", [P, 2, GROUP], F32)
-        table_offset = PACK * H * F32_BYTES
+        table_offset = PACK * H * F32_BYTES + LINE
         scale_table = reused.tile([P, T], U8, name="scale_table", offset=table_offset, align_bytes=64)
         word_table = sb("word_table", [P, T], U32, tag="words_then_wb_codes")
         words_hbm = x_words[0].rearrange("p c r -> p (c r)").bitcast(I32)
@@ -167,7 +167,7 @@ def tile_picked_selmom_none_po_kernel(
         wb_bf = [sb("wb_bf%d" % c, [P, SPAN], BF16) for c in range(N // P)]
         wb_c = sb("wb_c", [P, N], U32, tag="words_then_wb_codes")
         wb_s = sb("wb_s", [P, N], U8)
-        z2_bf = sb("z2_bf", [P, N * PACK], BF16)
+        z2_bf = [sb("z2_bf0", [P, HALF * PACK], BF16)]
         b_acc = []
 
         def quant_wb(c):
@@ -189,10 +189,10 @@ def tile_picked_selmom_none_po_kernel(
         for c in (1, 2):
             quant_wb(c)
             project_b(c)
-        weigh(z2_bf[:, block(0, SPAN)], b_acc[0], gi_t)
+        weigh(z2_bf[0][:, block(0, SPAN)], b_acc[0], gi_t)
         quant_wb(3)
         project_b(3)
-        weigh(z2_bf[:, block(1, SPAN)], b_acc[1], gi_t)
+        weigh(z2_bf[0][:, block(1, SPAN)], b_acc[1], gi_t)
 
         wa_bf = sb("wa_bf", [P, H * PACK], BF16, tag="rounded_wa_then_z2_codes")
         wa_c = sb("wa_c", [P, H], U32)
@@ -211,29 +211,29 @@ def tile_picked_selmom_none_po_kernel(
         for c in range(2):
             round_wa(nc.scalar.copy, c, 0, per_load)
 
-        weigh(z2_bf[:, block(2, SPAN)], b_acc[2], gi_t)
-        z2_s = [sb("z2_s%d" % h, [P, HALF], U8) for h in range(2)]
-        z2_c = [sb("z2_c0", [P, HALF], U32)]
         quant_half(0)
         a_acc = [project("bank_a0", wa_c, wa_s, 0)]
-        by_scalar = per_load - WA_BY_VECTOR
-        round_wa(nc.scalar.copy, 2, 0, per_load)
-        round_wa(nc.scalar.copy, 3, 0, by_scalar)
-        round_wa(nc.vector.tensor_copy, 3, by_scalar, per_load)
-        quant(z2_c[0], z2_s[0], slice(0, HALF), z2_bf[:, block(0, 2 * SPAN)])
+        z2_bf.append(reused.tile([P, HALF * PACK], BF16, name="z2_bf1", offset=HALF * F32_BYTES, align_bytes=64))
+        weigh(z2_bf[1][:, block(0, SPAN)], b_acc[2], gi_t)
+        z2_s = [sb("z2_s%d" % h, [P, HALF], U8) for h in range(2)]
+        z2_c = [reused.tile([P, HALF], U32, name="z2_c0", offset=3 * HALF * F32_BYTES, align_bytes=64)]
+        for c in (2, 3):
+            round_wa(nc.scalar.copy, c, 0, per_load)
+        quant(z2_c[0], z2_s[0], slice(0, HALF), z2_bf[0][:])
 
-        b_rows = reused.tile([P, PACK, P], BF16, name="b_rows", offset=2 * SPAN * F32_BYTES)
+        last_load = 3 * SPAN * F32_BYTES
+        b_rows = reused.tile([P, PACK, P], BF16, name="b_rows", offset=last_load + LINE - 2 * SPAN)
         for s in range(PACK):
             nc.scalar.activation(b_rows[:, s, :], b_acc[3][:, s, :], COPY, scale=gi_t[:, s : s + 1])
-        interleave(nc.scalar.copy, z2_bf[:, block(3, SPAN)], b_rows[:])
+        interleave(nc.scalar.copy, z2_bf[1][:, block(1, SPAN)], b_rows[:])
 
         quant_half(1)
         a_acc.append(project("bank_a1", wa_c, wa_s, 1))
         quant(wa_c, wa_s, slice(HALF, H), wa_bf[:, block(1, 2 * SPAN)])
         z2_c.append(sb("z2_c1", [P, HALF], U32, tag="rounded_wa_then_z2_codes"))
 
-        z_lo = reused.tile([P, HALF * PACK], BF16, name="z_lo", offset=3 * SPAN * F32_BYTES, align_bytes=64)
-        z_hi = sb("z_hi", [P, HALF * PACK], BF16, tag="z_then_result")
+        z_lo = reused.tile([P, HALF * PACK], BF16, name="z_lo", offset=last_load + LINE, align_bytes=64)
+        z_last = sb("z_last", [P, SPAN], BF16)
         z_c = sb("z_c", [P, H], U32)
         z_s = sb("z_s", [P, H], U8)
         last_class = project("bank_a3", wa_c, wa_s, 3)
@@ -250,7 +250,7 @@ def tile_picked_selmom_none_po_kernel(
                 MULT,
             )
 
-        tanh_cv = []
+        tanh_cv = {}
 
         def moments(t):
             cv = psum.tile([P, N], F32, name="bank_b%d" % t)
@@ -258,30 +258,33 @@ def tile_picked_selmom_none_po_kernel(
                 product(cv[:, block(h, HALF)], z_c, z_s, block(t), z2_c[h], z2_s[h], slice(0, HALF))
             whole_rows = sb("tanh_cv%d" % t, [P, N], F32)
             nc.scalar.activation(whole_rows[:], cv[:], TANH, bias=bias[:], scale=0.0625)
-            tanh_cv.append(whole_rows)
+            tanh_cv[t] = whole_rows
 
         weigh_half(0)
         weigh_half(1)
-        quant(z2_c[1], z2_s[1], slice(0, HALF), z2_bf[:, block(1, 2 * SPAN)])
-        for t in range(2):
-            quant(z_c, z_s, block(t), z_lo[:, block(t, SPAN)])
+        quant(z2_c[1], z2_s[1], slice(0, HALF), z2_bf[1][:])
+        def finish(t, interleaved):
+            quant(z_c, z_s, block(t), interleaved)
             moments(t)
-        weigh(z_hi[:, block(0, SPAN)], third_class, gt_t)
-        interleave(nc.vector.tensor_copy, z_hi[:, block(1, SPAN)], a_rows[:])
-        for t in range(2):
-            quant(z_c, z_s, block(2 + t), z_hi[:, block(t, SPAN)])
-            moments(2 + t)
 
-        y = sb("y", [P, PACK, V], F32, tag="z_then_result")
+        for t in range(2):
+            finish(t, z_lo[:, block(t, SPAN)])
+        z_third = reused.tile([P, SPAN], BF16, name="z_third", offset=last_load + LINE, align_bytes=64)
+        interleave(nc.vector.tensor_copy, z_last[:], a_rows[:])
+        weigh(z_third[:], third_class, gt_t)
+        finish(3, z_last[:])
+        finish(2, z_third[:])
+
+        y = reused.tile([P, PACK, V], F32, name="y", offset=last_load + LINE)
         out_rows = out_0.rearrange("(p t) v -> p t v", t=PACK)
-        last = PACK - 1
-        for t in range(last):
+        last = 2
+        for t in (0, 1, 3):
             nc.vector.tensor_copy(y[:, t, :], tanh_cv[t][:].indirect(cols_t[:]))
         nc.sync.dma_start(out_rows[:, 0:last, :], y[:, 0:last, :])
         halves = [tanh_cv[last][:].indirect(cols_t[:, block(h, P // GROUP)]) for h in range(2)]
         nc.scalar.activation(y[:, last, block(0)], halves[0], COPY)
         nc.vector.tensor_copy(y[:, last, block(1)], halves[1])
-        nc.sync.dma_start(out_rows[:, last, :], y[:, last, :])
+        nc.sync.dma_start(out_rows[:, last:PACK, :], y[:, last:PACK, :])
 
         y_bf = sb("y_bf", [P, V * PACK], BF16, tag="bias_then_rounded_result")
         y_c = sb("y_c", [P, V], U32)

@@ -32,7 +32,6 @@ RUN = 4
 BYTE_RUN = 16
 
 EARLY_WORDS = T // 8
-LINE = 64
 
 
 def tile_picked_selmom_none_po_kernel(
@@ -73,7 +72,7 @@ def tile_picked_selmom_none_po_kernel(
         offs_t = sb("offs_t", [P, S // GROUP], U16)
         cols_t = sb("cols_t", [P, V // GROUP], U16)
         gate_rows = sb("gate_rows", [P, 2, GROUP], F32)
-        table_offset = PACK * H * F32_BYTES + LINE
+        table_offset = PACK * H * F32_BYTES
         scale_table = reused.tile([P, T], U8, name="scale_table", offset=table_offset, align_bytes=64)
         word_table = sb("word_table", [P, T], U32, tag="words_then_wb_codes")
         words_hbm = x_words[0].rearrange("p c r -> p (c r)").bitcast(I32)
@@ -201,15 +200,15 @@ def tile_picked_selmom_none_po_kernel(
         wa_src = [raw.rearrange("p j (m t) -> p m j t", t=PACK) for raw in wa_raw]
         per_load = P // PACK
 
-        def round_wa(copy, c, first, last):
-            copy(wa_dealt[:, c * per_load + first : c * per_load + last], wa_src[c][:, first:last])
+        def round_wa(copy, c, classes):
+            copy(wa_dealt[:, block(c, per_load), :, classes], wa_src[c][:, :, :, classes])
 
         def quant_half(h):
             for t in range(2):
                 quant(wa_c, wa_s, block(2 * h + t, P // 2), wa_bf[:, block(2 * t + h, HALF)])
 
         for c in range(2):
-            round_wa(nc.scalar.copy, c, 0, per_load)
+            round_wa(nc.scalar.copy, c, slice(0, PACK))
 
         quant_half(0)
         a_acc = [project("bank_a0", wa_c, wa_s, 0)]
@@ -217,12 +216,13 @@ def tile_picked_selmom_none_po_kernel(
         weigh(z2_bf[1][:, block(0, SPAN)], b_acc[2], gi_t)
         z2_s = [sb("z2_s%d" % h, [P, HALF], U8) for h in range(2)]
         z2_c = [reused.tile([P, HALF], U32, name="z2_c0", offset=3 * HALF * F32_BYTES, align_bytes=64)]
-        for c in (2, 3):
-            round_wa(nc.scalar.copy, c, 0, per_load)
+        round_wa(nc.scalar.copy, 2, slice(0, PACK))
+        round_wa(nc.scalar.copy, 3, block(1, 2))
+        round_wa(nc.vector.tensor_copy, 3, block(0, 2))
         quant(z2_c[0], z2_s[0], slice(0, HALF), z2_bf[0][:])
 
         last_load = 3 * SPAN * F32_BYTES
-        b_rows = reused.tile([P, PACK, P], BF16, name="b_rows", offset=last_load + LINE - 2 * SPAN)
+        b_rows = reused.tile([P, PACK, P], BF16, name="b_rows", offset=2 * SPAN * F32_BYTES)
         for s in range(PACK):
             nc.scalar.activation(b_rows[:, s, :], b_acc[3][:, s, :], COPY, scale=gi_t[:, s : s + 1])
         interleave(nc.scalar.copy, z2_bf[1][:, block(1, SPAN)], b_rows[:])
@@ -232,7 +232,7 @@ def tile_picked_selmom_none_po_kernel(
         quant(wa_c, wa_s, slice(HALF, H), wa_bf[:, block(1, 2 * SPAN)])
         z2_c.append(sb("z2_c1", [P, HALF], U32, tag="rounded_wa_then_z2_codes"))
 
-        z_lo = reused.tile([P, HALF * PACK], BF16, name="z_lo", offset=last_load + LINE, align_bytes=64)
+        z_lo = reused.tile([P, HALF * PACK], BF16, name="z_lo", offset=last_load, align_bytes=64)
         z_last = sb("z_last", [P, SPAN], BF16)
         z_c = sb("z_c", [P, H], U32)
         z_s = sb("z_s", [P, H], U8)
@@ -269,13 +269,13 @@ def tile_picked_selmom_none_po_kernel(
 
         for t in range(2):
             finish(t, z_lo[:, block(t, SPAN)])
-        z_third = reused.tile([P, SPAN], BF16, name="z_third", offset=last_load + LINE, align_bytes=64)
+        z_third = reused.tile([P, SPAN], BF16, name="z_third", offset=last_load, align_bytes=64)
         interleave(nc.vector.tensor_copy, z_last[:], a_rows[:])
         weigh(z_third[:], third_class, gt_t)
         finish(3, z_last[:])
         finish(2, z_third[:])
 
-        y = reused.tile([P, PACK, V], F32, name="y", offset=last_load + LINE)
+        y = reused.tile([P, PACK, V], F32, name="y", offset=last_load)
         out_rows = out_0.rearrange("(p t) v -> p t v", t=PACK)
         last = 2
         for t in (0, 1, 3):

@@ -28,6 +28,10 @@ GROUP = 16
 QUADRANT = 32
 SCALE_ROWS = 4
 F32_BYTES = 4
+REGION = 32768
+SLOT = 2048
+LINE = 64
+BURST = 256
 RUN = 4
 BYTE_RUN = 16
 
@@ -41,10 +45,15 @@ def tile_picked_selmom_none_po_kernel(
     with ExitStack() as ctx:
         keep = ctx.enter_context(tc.tile_pool(name="keep", bufs=1))
         reused = ctx.enter_context(tc.tile_pool(name="reused", bufs=1))
+        apart = ctx.enter_context(tc.tile_pool(name="apart", bufs=1))
         psum = ctx.enter_context(tc.psum_pool(name="psum", bufs=1))
 
-        def sb(name, shape, dtype, tag=None):
-            return keep.tile(shape, dtype, name=name, tag=tag or name, align_bytes=64)
+        def sb(name, shape, dtype, tag=None, align=LINE):
+            return keep.tile(shape, dtype, name=name, tag=tag or name, align_bytes=align)
+
+        def far(name, shape, dtype, region, place):
+            offset = REGION // 2 + region * REGION + place * SLOT
+            return apart.tile(shape, dtype, name=name, offset=offset, align_bytes=BURST)
 
         def block(i, width=P):
             return slice(i * width, (i + 1) * width)
@@ -73,8 +82,8 @@ def tile_picked_selmom_none_po_kernel(
         cols_t = sb("cols_t", [P, V // GROUP], U16)
         gate_rows = sb("gate_rows", [P, 2, GROUP], F32)
         table_offset = PACK * H * F32_BYTES
-        scale_table = reused.tile([P, T], U8, name="scale_table", offset=table_offset, align_bytes=64)
-        word_table = sb("word_table", [P, T], U32, tag="words_then_wb_codes")
+        scale_table = reused.tile([P, T], U8, name="scale_table", offset=table_offset, align_bytes=BURST)
+        word_table = sb("word_table", [P, T], U32, tag="words_then_wb_codes", align=BURST)
         words_hbm = x_words[0].rearrange("p c r -> p (c r)").bitcast(I32)
 
         nc.vector.memset(scale_table[:].bitcast(I32), 0)
@@ -113,17 +122,17 @@ def tile_picked_selmom_none_po_kernel(
         def by_row(flat):
             return flat.rearrange("p (j c) -> p j c", j=PACK)
 
-        wb_first = by_row(sb("wb_first", [P, SPAN], F32)[:])
-        wb_middle = by_row(sb("wb_middle", [P, 2 * SPAN], F32)[:])
+        wb_first = by_row(far("wb_first", [P, SPAN], F32, 0, 1)[:])
+        wb_middle = by_row(far("wb_middle", [P, 2 * SPAN], F32, 2, 1)[:])
         nc.sync.dma_start(wb_first, wb_rows[:, :, block(0)])
         nc.sync.dma_start(wb_middle, wb_rows[:, :, P : 3 * P])
-        wb_last = by_row(sb("wb_last", [P, SPAN], F32)[:])
+        wb_last = by_row(far("wb_last", [P, SPAN], F32, 3, 1)[:])
         nc.sync.dma_start(wb_last, wb_rows[:, :, block(3)])
         wb_raw = [wb_first, wb_middle[:, :, block(0)], wb_middle[:, :, block(1)], wb_last]
 
-        picked_room = reused.tile([P, PACK * H * F32_BYTES], U8, name="picked_room", offset=0)
+        picked_room = reused.tile([P, PACK * H * F32_BYTES], U8, name="picked_room", offset=0, align_bytes=REGION)
         picked_scales = picked_room[:, 0:S]
-        x_s = sb("x_s", [P, S], U8)
+        x_s = sb("x_s", [P, S], U8, align=BURST)
         nc.vector.tensor_copy(picked_scales, scale_table[:].indirect(offs_t[:]))
         gates = reused.tile([P, 2 * PACK], F32, name="gates", offset=table_offset)
         gi_t, gt_t = gates[:, 0:PACK], gates[:, PACK : 2 * PACK]
@@ -139,13 +148,13 @@ def tile_picked_selmom_none_po_kernel(
 
         wa_raw = []
         for c in range(H // P):
-            raw = reused.tile([P, SPAN], F32, name="wa_raw%d" % c, offset=c * SPAN * F32_BYTES)
+            raw = reused.tile([P, SPAN], F32, name="wa_raw%d" % c, offset=c * SPAN * F32_BYTES, align_bytes=BURST)
             wa_raw.append(by_row(raw[:]))
             nc.sync.dma_start(wa_raw[c], wa_rows[:, :, block(c)])
 
         nc.sync.dma_start(cols_t[:], cols)
 
-        picked_words = reused.tile([P, S], U32, name="picked_words", offset=table_offset + 64, align_bytes=64)
+        picked_words = reused.tile([P, S], U32, name="picked_words", offset=table_offset + LINE, align_bytes=LINE)
         x_c = sb("x_c", [P, S], U32)
         nc.vector.tensor_copy(picked_words[:], word_table[:].indirect(offs_t[:]))
 
@@ -163,10 +172,10 @@ def tile_picked_selmom_none_po_kernel(
                 MULT,
             )
 
-        wb_bf = [sb("wb_bf%d" % c, [P, SPAN], BF16) for c in range(N // P)]
-        wb_c = sb("wb_c", [P, N], U32, tag="words_then_wb_codes")
+        wb_bf = [far("wb_bf%d" % c, [P, SPAN], BF16, 1, 3 + c) for c in range(N // P)]
+        wb_c = sb("wb_c", [P, N], U32, tag="words_then_wb_codes", align=BURST)
         wb_s = sb("wb_s", [P, N], U8)
-        z2_bf = [sb("z2_bf0", [P, HALF * PACK], BF16)]
+        z2_bf = [far("z2_bf0", [P, HALF * PACK], BF16, 0, 2)]
         b_acc = []
 
         def quant_wb(c):
@@ -193,7 +202,7 @@ def tile_picked_selmom_none_po_kernel(
         project_b(3)
         weigh(z2_bf[0][:, block(1, SPAN)], b_acc[1], gi_t)
 
-        wa_bf = sb("wa_bf", [P, H * PACK], BF16, tag="rounded_wa_then_z2_codes")
+        wa_bf = far("wa_bf", [P, H * PACK], BF16, 1, 1)
         wa_c = sb("wa_c", [P, H], U32)
         wa_s = sb("wa_s", [P, H], U8)
         wa_dealt = wa_bf[:].rearrange("p (t m j) -> p m j t", t=PACK, j=PACK)
@@ -212,10 +221,10 @@ def tile_picked_selmom_none_po_kernel(
 
         quant_half(0)
         a_acc = [project("bank_a0", wa_c, wa_s, 0)]
-        z2_bf.append(reused.tile([P, HALF * PACK], BF16, name="z2_bf1", offset=HALF * F32_BYTES, align_bytes=64))
+        z2_bf.append(reused.tile([P, HALF * PACK], BF16, name="z2_bf1", offset=HALF * F32_BYTES, align_bytes=LINE))
         weigh(z2_bf[1][:, block(0, SPAN)], b_acc[2], gi_t)
         z2_s = [sb("z2_s%d" % h, [P, HALF], U8) for h in range(2)]
-        z2_c = [reused.tile([P, HALF], U32, name="z2_c0", offset=3 * HALF * F32_BYTES, align_bytes=64)]
+        z2_c = [reused.tile([P, HALF], U32, name="z2_c0", offset=3 * HALF * F32_BYTES, align_bytes=LINE)]
         round_wa(nc.scalar.copy, 2, slice(0, PACK))
         round_wa(nc.scalar.copy, 3, block(1, 2))
         round_wa(nc.vector.tensor_copy, 3, block(0, 2))
@@ -230,14 +239,14 @@ def tile_picked_selmom_none_po_kernel(
         quant_half(1)
         a_acc.append(project("bank_a1", wa_c, wa_s, 1))
         quant(wa_c, wa_s, slice(HALF, H), wa_bf[:, block(1, 2 * SPAN)])
-        z2_c.append(sb("z2_c1", [P, HALF], U32, tag="rounded_wa_then_z2_codes"))
+        z2_c.append(far("z2_c1", [P, HALF], U32, 1, 1))
 
-        z_lo = reused.tile([P, HALF * PACK], BF16, name="z_lo", offset=last_load, align_bytes=64)
-        z_last = sb("z_last", [P, SPAN], BF16)
+        z_lo = reused.tile([P, HALF * PACK], BF16, name="z_lo", offset=last_load, align_bytes=LINE)
+        z_last = far("z_last", [P, SPAN], BF16, 2, 3)
         z_c = sb("z_c", [P, H], U32)
         z_s = sb("z_s", [P, H], U8)
         last_class = project("bank_a3", wa_c, wa_s, 3)
-        a_rows = sb("a_rows", [P, PACK, P], BF16)
+        a_rows = far("a_rows", [P, PACK, P], BF16, 3, 2)
         for s in range(PACK):
             nc.scalar.activation(a_rows[:, s, :], last_class[:, s, :], COPY, scale=gt_t[:, s : s + 1])
         third_class = project("bank_a2", wa_c, wa_s, 2)
@@ -256,7 +265,7 @@ def tile_picked_selmom_none_po_kernel(
             cv = psum.tile([P, N], F32, name="bank_b%d" % t)
             for h in range(2):
                 product(cv[:, block(h, HALF)], z_c, z_s, block(t), z2_c[h], z2_s[h], slice(0, HALF))
-            whole_rows = sb("tanh_cv%d" % t, [P, N], F32)
+            whole_rows = far("tanh_cv%d" % t, [P, N], F32, t, 0)
             nc.scalar.activation(whole_rows[:], cv[:], TANH, bias=bias[:], scale=0.0625)
             tanh_cv[t] = whole_rows
 
@@ -269,13 +278,13 @@ def tile_picked_selmom_none_po_kernel(
 
         for t in range(2):
             finish(t, z_lo[:, block(t, SPAN)])
-        z_third = reused.tile([P, SPAN], BF16, name="z_third", offset=last_load, align_bytes=64)
+        z_third = reused.tile([P, SPAN], BF16, name="z_third", offset=last_load, align_bytes=LINE)
         interleave(nc.vector.tensor_copy, z_last[:], a_rows[:])
         weigh(z_third[:], third_class, gt_t)
         finish(3, z_last[:])
         finish(2, z_third[:])
 
-        y = reused.tile([P, PACK, V], F32, name="y", offset=last_load)
+        y = reused.tile([P, PACK, V], F32, name="y", offset=last_load, align_bytes=BURST)
         out_rows = out_0.rearrange("(p t) v -> p t v", t=PACK)
         last = 2
         for t in (0, 1, 3):
@@ -287,8 +296,8 @@ def tile_picked_selmom_none_po_kernel(
         nc.sync.dma_start(out_rows[:, last:PACK, :], y[:, last:PACK, :])
 
         y_bf = sb("y_bf", [P, V * PACK], BF16, tag="bias_then_rounded_result")
-        y_c = sb("y_c", [P, V], U32)
-        y_s = sb("y_s", [P, V], U8)
+        y_c = sb("y_c", [P, V], U32, align=BURST)
+        y_s = sb("y_s", [P, V], U8, align=BURST)
         interleave(nc.scalar.copy, y_bf[:, block(0, SPAN)], y[:, :, block(0)])
         interleave(nc.vector.tensor_copy, y_bf[:, block(1, SPAN)], y[:, :, block(1)])
         for h in (1, 0):

@@ -58,16 +58,29 @@ def tile_picked_selmom_none_po_kernel(
         def block(i, width=P):
             return slice(i * width, (i + 1) * width)
 
+        def scale_plane(name, columns, run):
+            pitch = run + P if run > P else BURST
+            plane = sb(name, [P, columns // run * pitch], U8, align=BURST)
+
+            def view(wanted):
+                start = wanted.start // run * pitch + P + wanted.start % run
+                return plane[:, start : start + wanted.stop - wanted.start]
+
+            return view
+
+        def plain(plane):
+            return lambda wanted: plane[:, wanted]
+
         def quant(codes, scales, columns, interleaved):
-            nc.vector.quantize_mx(out=codes[:, columns].bitcast(FP8X4), scales=scales[:, columns], in_=interleaved)
+            nc.vector.quantize_mx(out=codes[:, columns].bitcast(FP8X4), scales=scales(columns), in_=interleaved)
 
         def product(out, lhs_codes, lhs_scales, lhs_columns, rhs_codes, rhs_scales, rhs_columns):
             nc.tensor.matmul_mx(
                 out=out,
                 lhsT=lhs_codes[:, lhs_columns].bitcast(FP8X4),
-                lhsT_scale=lhs_scales[:, lhs_columns],
+                lhsT_scale=lhs_scales(lhs_columns),
                 rhs=rhs_codes[:, rhs_columns].bitcast(FP8X4),
-                rhs_scale=rhs_scales[:, rhs_columns],
+                rhs_scale=rhs_scales(rhs_columns),
                 start=True,
                 stop=True,
             )
@@ -155,13 +168,13 @@ def tile_picked_selmom_none_po_kernel(
         nc.sync.dma_start(cols_t[:], cols)
 
         picked_words = reused.tile([P, S], U32, name="picked_words", offset=table_offset + LINE, align_bytes=LINE)
-        x_c = sb("x_c", [P, S], U32)
+        x_c = sb("x_c", [P, S], U32, align=BURST)
         nc.vector.tensor_copy(picked_words[:], word_table[:].indirect(offs_t[:]))
 
         def project(bank, codes, scales, c):
             acc = psum.tile([P, PACK, P], F32, name=bank)
             for s in range(PACK):
-                product(acc[:, s, :], x_c, x_s, block(s), codes, scales, block(c))
+                product(acc[:, s, :], x_c, plain(x_s), block(s), codes, scales, block(c))
             return acc
 
         def weigh(interleaved, acc, gate):
@@ -174,7 +187,7 @@ def tile_picked_selmom_none_po_kernel(
 
         wb_bf = [far("wb_bf%d" % c, [P, SPAN], BF16, 1, 3 + c) for c in range(N // P)]
         wb_c = sb("wb_c", [P, N], U32, tag="words_then_wb_codes", align=BURST)
-        wb_s = sb("wb_s", [P, N], U8)
+        wb_s = scale_plane("wb_s", N, P)
         z2_bf = [far("z2_bf0", [P, HALF * PACK], BF16, 0, 2)]
         b_acc = []
 
@@ -203,8 +216,8 @@ def tile_picked_selmom_none_po_kernel(
         weigh(z2_bf[0][:, block(1, SPAN)], b_acc[1], gi_t)
 
         wa_bf = far("wa_bf", [P, H * PACK], BF16, 1, 1)
-        wa_c = sb("wa_c", [P, H], U32)
-        wa_s = sb("wa_s", [P, H], U8)
+        wa_c = sb("wa_c", [P, H], U32, align=BURST)
+        wa_s = scale_plane("wa_s", H, P)
         wa_dealt = wa_bf[:].rearrange("p (t m j) -> p m j t", t=PACK, j=PACK)
         wa_src = [raw.rearrange("p j (m t) -> p m j t", t=PACK) for raw in wa_raw]
         per_load = P // PACK
@@ -223,7 +236,7 @@ def tile_picked_selmom_none_po_kernel(
         a_acc = [project("bank_a0", wa_c, wa_s, 0)]
         z2_bf.append(reused.tile([P, HALF * PACK], BF16, name="z2_bf1", offset=HALF * F32_BYTES, align_bytes=LINE))
         weigh(z2_bf[1][:, block(0, SPAN)], b_acc[2], gi_t)
-        z2_s = [sb("z2_s%d" % h, [P, HALF], U8) for h in range(2)]
+        z2_s = [scale_plane("z2_s%d" % h, HALF, HALF) for h in range(2)]
         z2_c = [reused.tile([P, HALF], U32, name="z2_c0", offset=3 * HALF * F32_BYTES, align_bytes=LINE)]
         round_wa(nc.scalar.copy, 2, slice(0, PACK))
         round_wa(nc.scalar.copy, 3, block(1, 2))
@@ -238,13 +251,14 @@ def tile_picked_selmom_none_po_kernel(
 
         quant_half(1)
         a_acc.append(project("bank_a1", wa_c, wa_s, 1))
-        quant(wa_c, wa_s, slice(HALF, H), wa_bf[:, block(1, 2 * SPAN)])
+        for t in (3, 2):
+            quant(wa_c, wa_s, block(t), wa_bf[:, block(t, SPAN)])
         z2_c.append(far("z2_c1", [P, HALF], U32, 1, 1))
 
         z_lo = reused.tile([P, HALF * PACK], BF16, name="z_lo", offset=last_load, align_bytes=LINE)
         z_last = far("z_last", [P, SPAN], BF16, 2, 3)
-        z_c = sb("z_c", [P, H], U32)
-        z_s = sb("z_s", [P, H], U8)
+        z_c = sb("z_c", [P, H], U32, align=BURST)
+        z_s = scale_plane("z_s", H, P)
         last_class = project("bank_a3", wa_c, wa_s, 3)
         a_rows = far("a_rows", [P, PACK, P], BF16, 3, 2)
         for s in range(PACK):
@@ -301,7 +315,7 @@ def tile_picked_selmom_none_po_kernel(
         interleave(nc.scalar.copy, y_bf[:, block(0, SPAN)], y[:, :, block(0)])
         interleave(nc.vector.tensor_copy, y_bf[:, block(1, SPAN)], y[:, :, block(1)])
         for h in (1, 0):
-            quant(y_c, y_s, block(h), y_bf[:, block(h, SPAN)])
+            quant(y_c, plain(y_s), block(h), y_bf[:, block(h, SPAN)])
         nc.sync.dma_start(out_1[0].rearrange("p c r -> p (c r)").bitcast(I32), y_c[:].bitcast(I32))
         for q in range(P // QUADRANT):
             queue = nc.scalar if q % 2 == 0 else nc.sync

from contextlib import ExitStack

import concourse.mybir as mybir

K, T, S, V, N, H = 512, 2048, 512, 256, 512, 512
FLOPS = 2 * K * S * H + 2 * K * S * N + 2 * S * H * N

F32 = mybir.dt.float32
BF16 = mybir.dt.bfloat16
I32 = mybir.dt.int32
U32 = mybir.dt.uint32
U16 = mybir.dt.uint16
U8 = mybir.dt.uint8
FP8X4 = mybir.dt.float8_e4m3fn_x4
TANH = mybir.ActivationFunctionType.Tanh
COPY = mybir.ActivationFunctionType.Copy
MULT = mybir.AluOpType.mult
ADD = mybir.AluOpType.add
EQUAL = mybir.AluOpType.is_equal
AXIS_X = mybir.AxisListType.X

P = 128
PACK = 4
HALF = 256
SPAN = P * PACK
BLOCK = 32
GROUP = 16
QUADRANT = 32
SCALE_ROWS = 4
F32_BYTES = 4
REGION = 32768
SLOT = 2048
LINE = 64
BURST = 256
RUN = 4
BYTE_RUN = 16

EARLY_WORDS = T // 8


def tile_picked_selmom_none_po_kernel(
    tc, x_words, x_scales, wa, wb, gt, gi, offs, cols, out_0, out_1, out_2
):
    nc = tc.nc
    with ExitStack() as ctx:
        keep = ctx.enter_context(tc.tile_pool(name="keep", bufs=1))
        reused = ctx.enter_context(tc.tile_pool(name="reused", bufs=1))
        apart = ctx.enter_context(tc.tile_pool(name="apart", bufs=1))
        psum = ctx.enter_context(tc.psum_pool(name="psum", bufs=1))

        def sb(name, shape, dtype, tag=None, align=LINE):
            return keep.tile(shape, dtype, name=name, tag=tag or name, align_bytes=align)

        def far(name, shape, dtype, region, place):
            offset = REGION // 2 + region * REGION + place * SLOT
            return apart.tile(shape, dtype, name=name, offset=offset, align_bytes=BURST)

        def block(i, width=P):
            return slice(i * width, (i + 1) * width)

        def scale_plane(name, columns, run):
            pitch = run + P if run > P else BURST
            plane = sb(name, [P, columns // run * pitch], U8, align=BURST)

            def view(wanted):
                start = wanted.start // run * pitch + P + wanted.start % run
                return plane[:, start : start + wanted.stop - wanted.start]

            return view

        def plain(plane):
            return lambda wanted: plane[:, wanted]

        def quant(codes, scales, columns, interleaved):
            nc.vector.quantize_mx(out=codes[:, columns].bitcast(FP8X4), scales=scales(columns), in_=interleaved)

        def product(out, lhs_codes, lhs_scales, lhs_columns, rhs_codes, rhs_scales, rhs_columns):
            nc.tensor.matmul_mx(
                out=out,
                lhsT=lhs_codes[:, lhs_columns].bitcast(FP8X4),
                lhsT_scale=lhs_scales(lhs_columns),
                rhs=rhs_codes[:, rhs_columns].bitcast(FP8X4),
                rhs_scale=rhs_scales(rhs_columns),
                start=True,
                stop=True,
            )

        def interleave(copy, interleaved, rows):
            copy(
                interleaved.rearrange("p (c i j) -> p c j i", i=RUN, j=PACK),
                rows.rearrange("p j (c i) -> p c j i", i=RUN),
            )

        offs_t = sb("offs_t", [P, S // GROUP], U16)
        cols_t = sb("cols_t", [P, V // GROUP], U16)
        gate_rows = sb("gate_rows", [P, 2, GROUP], F32)
        table_offset = PACK * H * F32_BYTES
        scale_table = reused.tile([P, T], U8, name="scale_table", offset=table_offset, align_bytes=BURST)
        word_table = sb("word_table", [P, T], U32, tag="words_then_wb_codes", align=BURST)
        words_hbm = x_words[0].rearrange("p c r -> p (c r)").bitcast(I32)

        nc.vector.memset(scale_table[:].bitcast(I32), 0)
        nc.sync.dma_start(offs_t[:], offs)
        for i, gate in enumerate((gi, gt)):
            sixteen = gate.rearrange("(q u e) o -> q u (e o)", u=1, e=GROUP)
            nc.scalar.dma_start(gate_rows[:, i, :], sixteen.broadcast_to([P // RUN, RUN, GROUP]))
        nc.sync.dma_start(word_table[:, 0:EARLY_WORDS].bitcast(I32), words_hbm[:, 0:EARLY_WORDS])
        for odd, queue in enumerate((nc.sync, nc.scalar)):
            queue.dma_start(scale_table[odd:P:GROUP, :].bitcast(I32), x_scales[0][odd : K // BLOCK : 2, :].bitcast(I32))
        nc.sync.dma_start(word_table[:, EARLY_WORDS:T].bitcast(I32), words_hbm[:, EARLY_WORDS:T])

        column_rest = sb("column_rest", [P, QUADRANT], F32)
        partition_rest = sb("partition_rest", [P, QUADRANT], F32)
        own = sb("own", [P, RUN], F32)
        masked = sb("masked", [P, 2 * PACK, RUN], F32)
        for r in range(RUN):
            nc.vector.memset(column_rest[:, r:QUADRANT:RUN], float(r))
        nc.vector.transpose(partition_rest[:], column_rest[:])
        nc.vector.tensor_tensor(own[:], partition_rest[:, 0:RUN], column_rest[:, 0:RUN], EQUAL)
        nc.vector.tensor_tensor(
            masked[:],
            gate_rows[:].rearrange("p g (s r) -> p (g s) r", r=RUN),
            own[:].rearrange("p (o r) -> p o r", o=1).broadcast_to([P, 2 * PACK, RUN]),
            MULT,
        )

        zero = sb("zero", [P, 1], F32)
        bias = sb("bias", [P, 1], F32, tag="bias_then_rounded_result")
        nc.vector.memset(zero[:], 0.0)
        nc.scalar.activation(bias[:], zero[:], TANH)

        wb_rows = wb.rearrange("(p j) c -> p j c", j=PACK)
        wa_rows = wa.rearrange("(p j) c -> p j c", j=PACK)

        def by_row(flat):
            return flat.rearrange("p (j c) -> p j c", j=PACK)

        wb_first = by_row(far("wb_first", [P, SPAN], F32, 0, 1)[:])
        wb_middle = by_row(far("wb_middle", [P, 2 * SPAN], F32, 2, 1)[:])
        nc.sync.dma_start(wb_first, wb_rows[:, :, block(0)])
        nc.sync.dma_start(wb_middle, wb_rows[:, :, P : 3 * P])
        wb_last = by_row(far("wb_last", [P, SPAN], F32, 3, 1)[:])
        nc.sync.dma_start(wb_last, wb_rows[:, :, block(3)])
        wb_raw = [wb_first, wb_middle[:, :, block(0)], wb_middle[:, :, block(1)], wb_last]

        picked_room = reused.tile([P, PACK * H * F32_BYTES], U8, name="picked_room", offset=0, align_bytes=REGION)
        picked_scales = picked_room[:, 0:S]
        x_s = sb("x_s", [P, S], U8, align=BURST)
        nc.vector.tensor_copy(picked_scales, scale_table[:].indirect(offs_t[:]))
        gates = reused.tile([P, 2 * PACK], F32, name="gates", offset=table_offset)
        gi_t, gt_t = gates[:, 0:PACK], gates[:, PACK : 2 * PACK]
        nc.vector.tensor_reduce(gates[:], masked[:], AXIS_X, ADD)
        nc.vector.tensor_copy(
            x_s[:].bitcast(I32).rearrange("p (s q) -> p s q", s=PACK),
            picked_scales.bitcast(I32).rearrange("p (q s) -> p s q", s=PACK),
        )
        for odd, queue in enumerate((nc.sync, nc.scalar)):
            queue.dma_start(
                x_s[2 + odd : P : QUADRANT, :].bitcast(I32), x_s[GROUP + odd : P : QUADRANT, :].bitcast(I32)
            )

        wa_raw = []
        for c in range(H // P):
            raw = reused.tile([P, SPAN], F32, name="wa_raw%d" % c, offset=c * SPAN * F32_BYTES, align_bytes=BURST)
            wa_raw.append(by_row(raw[:]))
            nc.sync.dma_start(wa_raw[c], wa_rows[:, :, block(c)])

        nc.sync.dma_start(cols_t[:], cols)

        picked_words = reused.tile([P, S], U32, name="picked_words", offset=table_offset + LINE, align_bytes=LINE)
        x_c = sb("x_c", [P, S], U32, align=BURST)
        nc.vector.tensor_copy(picked_words[:], word_table[:].indirect(offs_t[:]))

        def project(bank, codes, scales, c):
            acc = psum.tile([P, PACK, P], F32, name=bank)
            for s in range(PACK):
                product(acc[:, s, :], x_c, plain(x_s), block(s), codes, scales, block(c))
            return acc

        def weigh(interleaved, acc, gate):
            nc.vector.tensor_tensor(
                interleaved.rearrange("p (m s) -> p m s", s=PACK),
                acc[:].rearrange("p s m -> p m s"),
                gate.rearrange("p (o s) -> p o s", o=1).broadcast_to([P, P, PACK]),
                MULT,
            )

        wb_bf = [far("wb_bf%d" % c, [P, SPAN], BF16, 1, 3 + c) for c in range(N // P)]
        wb_c = sb("wb_c", [P, N], U32, tag="words_then_wb_codes", align=BURST)
        wb_s = scale_plane("wb_s", N, P)
        z2_bf = [far("z2_bf0", [P, HALF * PACK], BF16, 0, 2)]
        b_acc = []

        def quant_wb(c):
            quant(wb_c, wb_s, block(c), wb_bf[c][:])

        def project_b(c):
            b_acc.append(project("bank_b%d" % c, wb_c, wb_s, c))

        for c in (0, 1, 3):
            interleave(nc.scalar.copy, wb_bf[c][:], wb_raw[c])
        quant_wb(0)
        for u in range(2):
            nc.vector.tensor_copy(
                x_c[:].bitcast(I32).rearrange("p (s q r) -> p q s r", s=PACK, r=RUN)[:, :, block(u, 2)],
                picked_words[:].bitcast(I32).rearrange("p (q s r) -> p q s r", s=PACK, r=RUN)[:, :, block(u, 2)],
            )
        project_b(0)
        interleave(nc.vector.tensor_copy, wb_bf[2][:], wb_raw[2])
        for c in (1, 2):
            quant_wb(c)
            project_b(c)
        weigh(z2_bf[0][:, block(0, SPAN)], b_acc[0], gi_t)
        quant_wb(3)
        project_b(3)
        weigh(z2_bf[0][:, block(1, SPAN)], b_acc[1], gi_t)

        wa_bf = far("wa_bf", [P, H * PACK], BF16, 1, 1)
        wa_c = sb("wa_c", [P, H], U32, align=BURST)
        wa_s = scale_plane("wa_s", H, P)
        wa_dealt = wa_bf[:].rearrange("p (t m j) -> p m j t", t=PACK, j=PACK)
        wa_src = [raw.rearrange("p j (m t) -> p m j t", t=PACK) for raw in wa_raw]
        per_load = P // PACK

        def round_wa(copy, c, classes):
            copy(wa_dealt[:, block(c, per_load), :, classes], wa_src[c][:, :, :, classes])

        def quant_half(h):
            for t in range(2):
                quant(wa_c, wa_s, block(2 * h + t, P // 2), wa_bf[:, block(2 * t + h, HALF)])

        for c in range(2):
            round_wa(nc.scalar.copy, c, slice(0, PACK))

        quant_half(0)
        a_acc = [project("bank_a0", wa_c, wa_s, 0)]
        z2_bf.append(reused.tile([P, HALF * PACK], BF16, name="z2_bf1", offset=HALF * F32_BYTES, align_bytes=LINE))
        weigh(z2_bf[1][:, block(0, SPAN)], b_acc[2], gi_t)
        z2_s = [scale_plane("z2_s%d" % h, HALF, HALF) for h in range(2)]
        z2_c = [reused.tile([P, HALF], U32, name="z2_c0", offset=3 * HALF * F32_BYTES, align_bytes=LINE)]
        round_wa(nc.scalar.copy, 2, slice(0, PACK))
        round_wa(nc.scalar.copy, 3, block(1, 2))
        round_wa(nc.vector.tensor_copy, 3, block(0, 2))
        quant(z2_c[0], z2_s[0], slice(0, HALF), z2_bf[0][:])

        last_load = 3 * SPAN * F32_BYTES
        b_rows = reused.tile([P, PACK, P], BF16, name="b_rows", offset=2 * SPAN * F32_BYTES)
        for s in range(PACK):
            nc.scalar.activation(b_rows[:, s, :], b_acc[3][:, s, :], COPY, scale=gi_t[:, s : s + 1])
        interleave(nc.scalar.copy, z2_bf[1][:, block(1, SPAN)], b_rows[:])

        quant_half(1)
        a_acc.append(project("bank_a1", wa_c, wa_s, 1))
        for t in (3, 2):
            quant(wa_c, wa_s, block(t), wa_bf[:, block(t, SPAN)])
        z2_c.append(far("z2_c1", [P, HALF], U32, 1, 1))

        z_lo = reused.tile([P, HALF * PACK], BF16, name="z_lo", offset=last_load, align_bytes=LINE)
        z_last = far("z_last", [P, SPAN], BF16, 2, 3)
        z_c = sb("z_c", [P, H], U32, align=BURST)
        z_s = scale_plane("z_s", H, P)
        last_class = project("bank_a3", wa_c, wa_s, 3)
        a_rows = far("a_rows", [P, PACK, P], BF16, 3, 2)
        for s in range(PACK):
            nc.scalar.activation(a_rows[:, s, :], last_class[:, s, :], COPY, scale=gt_t[:, s : s + 1])
        third_class = project("bank_a2", wa_c, wa_s, 2)

        def weigh_half(h):
            nc.vector.tensor_tensor(
                z_lo[:].rearrange("p (b h m s) -> p h b m s", b=2, h=2, s=PACK)[:, h],
                a_acc[h][:].rearrange("p s (b m) -> p b m s", b=2),
                gt_t.rearrange("p (b m s) -> p b m s", b=1, m=1).broadcast_to([P, 2, P // 2, PACK]),
                MULT,
            )

        tanh_cv = {}

        def moments(t):
            cv = psum.tile([P, N], F32, name="bank_b%d" % t)
            for h in range(2):
                product(cv[:, block(h, HALF)], z_c, z_s, block(t), z2_c[h], z2_s[h], slice(0, HALF))
            whole_rows = far("tanh_cv%d" % t, [P, N], F32, t, 0)
            nc.scalar.activation(whole_rows[:], cv[:], TANH, bias=bias[:], scale=0.0625)
            tanh_cv[t] = whole_rows

        weigh_half(0)
        weigh_half(1)
        quant(z2_c[1], z2_s[1], slice(0, HALF), z2_bf[1][:])
        def finish(t, interleaved):
            quant(z_c, z_s, block(t), interleaved)
            moments(t)

        for t in range(2):
            finish(t, z_lo[:, block(t, SPAN)])
        z_third = reused.tile([P, SPAN], BF16, name="z_third", offset=last_load, align_bytes=LINE)
        interleave(nc.vector.tensor_copy, z_last[:], a_rows[:])
        weigh(z_third[:], third_class, gt_t)
        finish(3, z_last[:])
        finish(2, z_third[:])

        y = reused.tile([P, PACK, V], F32, name="y", offset=last_load, align_bytes=BURST)
        out_rows = out_0.rearrange("(p t) v -> p t v", t=PACK)
        last = 2
        for t in (0, 1, 3):
            nc.vector.tensor_copy(y[:, t, :], tanh_cv[t][:].indirect(cols_t[:]))
        nc.sync.dma_start(out_rows[:, 0:last, :], y[:, 0:last, :])
        halves = [tanh_cv[last][:].indirect(cols_t[:, block(h, P // GROUP)]) for h in range(2)]
        nc.scalar.activation(y[:, last, block(0)], halves[0], COPY)
        nc.vector.tensor_copy(y[:, last, block(1)], halves[1])
        nc.sync.dma_start(out_rows[:, last:PACK, :], y[:, last:PACK, :])

        y_bf = sb("y_bf", [P, V * PACK], BF16, tag="bias_then_rounded_result")
        y_c = sb("y_c", [P, V], U32, align=BURST)
        y_s = sb("y_s", [P, V], U8, align=BURST)
        interleave(nc.scalar.copy, y_bf[:, block(0, SPAN)], y[:, :, block(0)])
        interleave(nc.vector.tensor_copy, y_bf[:, block(1, SPAN)], y[:, :, block(1)])
        for h in (1, 0):
            quant(y_c, plain(y_s), block(h), y_bf[:, block(h, SPAN)])
        nc.sync.dma_start(out_1[0].rearrange("p c r -> p (c r)").bitcast(I32), y_c[:].bitcast(I32))
        for q in range(P // QUADRANT):
            queue = nc.scalar if q % 2 == 0 else nc.sync
            queue.dma_start(
                out_2[0][block(q, SCALE_ROWS), :].bitcast(I32),
                y_s[QUADRANT * q : QUADRANT * q + SCALE_ROWS, :].bitcast(I32),
            )
